import numpy as np, ml_dtypes
CORES = [23,119,17,113]
N = 4
BF = ml_dtypes.bfloat16
W, LN, HO, TH = 4096, 256, 6, 64
def spot(a, s, k):
    return ((a * s >> 5) + a + 37 * s + k) & (W - 1)
def parts(rng):
    return (rng.integers(0, 16, (N, 8, 16, W)), rng.integers(0, W, (N, 8, 16, LN)), rng.integers(0, 16, (N, 8, 16, LN)), rng.integers(0, 16, (N, 8, 16, LN)),
            rng.integers(0, W, (N, 8, LN)), rng.integers(0, W, (N, 8, 16)))
def pack(X, P, A, R, s, K):
    b = lambda v, n: np.ascontiguousarray(np.reshape(v, (N, 128, n))).astype(np.float32).astype(BF)
    return {"x": b(X, W), "pn": np.ascontiguousarray(P.reshape(N, 128, LN)).astype(np.int32), "a0": b(A, LN), "r0": b(R, LN),
            "s0": np.ascontiguousarray(s).astype(np.int32), "kap": np.ascontiguousarray(K.reshape(N, 128, 1)).astype(np.int32)}
def setup_inputs(rng):
    return pack(*parts(rng))
def setup_inputs_spread(rng):
    X, P, A, R, s, K = parts(rng); lg = W.bit_length() - 1
    def small(n):
        top = rng.integers(0, 16, (N, 8, 1, n)); return np.minimum((rng.random((N, 8, 16, n)) * (top + 1)).astype(np.int64), top)
    def skew(*sh):
        v = np.minimum(np.exp2(lg * rng.random(sh)).astype(np.int64) - 1, W - 1); return np.where(rng.random(sh) < 0.5, v, W - 1 - v)
    X, P, A, R, s, K = small(W), skew(N, 8, 16, LN), small(LN), small(LN), skew(N, 8, LN), skew(N, 8, 16)
    pairs = ((3, 21), (21, 3), (5, 19), (19, 5), (7, 9), (9, 7))
    for q in range(N):
        for g in range(0, 8, 2):
            u, v = pairs[int(rng.integers(0, 6))]; l = int(rng.integers(0, LN))
            s[q, g, l] = W - u; K[q, g] = (W - v - spot(P[q, g, :, l], W - u, 0)) & (W - 1)
    return pack(X, P, A, R, s, K)
def setup_inputs_ends(rng):
    e = W - 1; bit = lambda *sh: rng.integers(0, 2, sh)
    def ends(n):
        v = 15 * bit(N, 8, 16, n); return np.where(rng.random((N, 8, 1, n)) < 0.5, v[:, :, :1], v)
    X, A, R = ends(W), ends(LN), ends(LN); P, s, K = e * bit(N, 8, 16, LN), e * bit(N, 8, LN), e * bit(N, 8, 16)
    K[:, :, 15] = 0; K[:, :, 14] = e
    for l in (0, 1, 6, LN - 2, LN - 1): P[..., l] = e; s[..., l] = e
    s[..., 3] = 0; s[..., LN - 3] = 0
    lo = sorted(set(spot(a, 0, k) for a in (0, e) for k in (0, e))); hi = sorted(set(spot(a, e, k) for a in (0, e) for k in (0, e)))
    w = bit(N, 8, 1, 1); o = rng.permutation(N - 1)
    for q, far in ((N - 1, 1), (int(o[0]), 0), (int(o[1]), 1)):
        X[q][:, :, lo] = 15 * w[q]; X[q][:, :, hi] = 15 * (1 - w[q])
        A[q] = 15 * ((w[q] + (s[q][:, None, :] > 0) + far) & 1)
    c = int(o[1]); A[c, 7, :, LN - 1] = 15 - A[c, 7, :, LN - 1]
    return pack(X, P, A, R, s, K)
def setup_inputs_corners(rng):
    X, P, A, R, s, K = parts(rng); off = int(rng.integers(0, 4)); H = W // 2; row = np.arange(16)[:, None]
    for q in range(N):
        for g in range(8):
            m = (q + g + off) % 4
            if m == 0:
                c = rng.integers(0, 16, (16, 1)); X[q, g] = c; A[q, g] = c; R[q, g] = c
            elif m == 1:
                c = 15 * int(rng.integers(0, 2)); X[q, g] = c; A[q, g] = 15 - c; R[q, g] = 15 - c
                if g >= 4:
                    s[q, g] = int(rng.integers(0, 32)); P[q, g, 0] = rng.permutation(H)[:LN]
            elif m == 2:
                c = 15 * int(rng.integers(0, 2)); X[q, g, :, :H] = c; X[q, g, :, H:] = 15 - c; A[q, g] = c; R[q, g] = np.where(rng.random(LN) < 0.5, c, 15 - c)
                kind = rng.integers(0, 8, LN); kind[:8] = np.arange(8); kind[LN - 8:] = rng.permutation(8)
                rows = row + np.zeros((1, LN), np.int64)
                mk = np.stack([rows < 0, rows == 0, rows == 15, (rows == 0) | (rows == 15), rows < 15, rows == rng.integers(0, 16, (1, LN)), rows >= 0, rows == 14])
                near = mk[kind, :, np.arange(LN)].T
                site = np.where(rng.random((16, LN)) < 0.3, (H - 1) * rng.integers(0, 2, (16, LN)), rng.integers(0, H, (16, LN))) + np.where(near, 0, H)
                s[q, g] = 0; P[q, g] = (site - K[q, g][:, None]) & (W - 1)
            else:
                s[q, g] = rng.choice(np.array([0, 1, H, W - 1]), LN); K[q, g] = (W - 1) * rng.integers(0, 2, 16)
                P[q, g] = np.where(rng.random((16, LN)) < 0.4, s[q, g][None, :], (W - 1) * rng.integers(0, 2, (16, LN)))
    return pack(X, P, A, R, s, K)
def setup_inputs_crowd(rng):
    X, P, A, R, s, K = parts(rng); h = LN // 2
    P[:, 3] = P[:, 3, :1]
    P[:, ::2] = P[:, ::2, :, :1].copy(); s[:, ::2] = s[:, ::2, :1].copy()
    P[:, 1:7:2, :, h:] = P[:, 1:7:2, :, :h][..., ::-1].copy(); s[:, 1:7:2, h:] = s[:, 1:7:2, :h][..., ::-1].copy()
    P[:, 7, :, 1::2] = P[:, 7, :, ::2].copy(); s[:, 7, 1::2] = s[:, 7, ::2].copy()
    for g in (0, 6):
        A[:, g] = rng.integers(8, 16, (N, 16, LN))
        for q in range(N): X[q, g][:, spot(P[q, g, :, 0], s[q, g, 0], K[q, g])] = 0
    return pack(X, P, A, R, s, K)
def gaps(rng):
    n = np.where(rng.random((N, 8, 1, LN)) < 0.4, TH - 1, TH + rng.integers(0, 17, (N, 8, 1, LN))); n[..., 0] = TH; n[..., LN - 1] = TH - 1
    return n
def dist(rng, z, n):
    i = np.argsort(rng.random((N, 8, 16, LN)), axis=2)
    return np.abs(z - ((n + i) >> 4))
def setup_inputs_ties(rng):
    X, P, A, R, s, K = parts(rng)
    z = 15 * rng.integers(0, 2, (N, 8, 1, W)); z[:, ::2] = z[:, ::2, :, :1].copy()
    zl = 15 * rng.integers(0, 2, (N, 8, 1, LN)); zl[:, ::2] = z[:, ::2, :, :1]
    c = int(rng.integers(0, N)); b = (c - 1) % N; a = (c - 2) % N
    zc = 15 * ((np.arange(8) // 2 + int(rng.integers(0, 2))) & 1)[:, None, None]
    z[c] = zc
    for q in (a, b): z[q, ::2] = zc[::2]
    for q in (a, b, c): zl[q] = zc
    na, nr = gaps(rng), gaps(rng)
    na[b] = TH - 1; nr[b] = TH - 1; na[c] = TH - 1; na[c, :, 0, 0] = TH
    e = int(rng.integers(1, 8)); gs = rng.integers(0, 8, e); ls = 1 + rng.permutation(LN - 2)[:e]
    na[c, gs, 0, ls] = TH + rng.integers(0, 17, e)
    X[:] = z
    return pack(X, P, dist(rng, zl, na), dist(rng, zl, nr), s, K)
def check_inputs(d):
    bad = []
    for k, lo, hi in (("x", 0, 15), ("pn", 0, W - 1), ("a0", 0, 15), ("r0", 0, 15), ("s0", 0, W - 1), ("kap", 0, W - 1)):
        v = np.asarray(d[k]).astype(np.float64)
        if not np.all((v >= lo) & (v <= hi) & (v == np.floor(v))): bad.append("range of " + k)
    return bad
def reference(x, pn, a0, r0, s0, kap):
    X = x.astype(np.float32).astype(np.int64).reshape(N, 8, 16, W); P = pn.astype(np.int64).reshape(N, 8, 16, LN)
    A = a0.astype(np.float32).astype(np.int64).reshape(N, 8, 16, LN); R = r0.astype(np.float32).astype(np.int64).reshape(N, 8, 16, LN)
    s = s0.astype(np.int64); K = kap.astype(np.int64).reshape(N, 8, 16, 1)
    p = np.zeros((N, 8, LN), np.int64); ex = np.zeros((N, 8, LN), np.int64); missed = np.zeros(N, np.int64); row = np.arange(16)[:, None]
    for t in range(HO):
        last = missed; missed = np.zeros(N, np.int64)
        for r in range(N):
            q = (r + t) % N
            h = spot(P[r], s[r][:, None, :], K[q])
            v = np.take_along_axis(X[q], h.reshape(8, 1, 16 * LN), 2).reshape(8, 16, 16, LN)
            dd = np.add.reduce(np.abs(v - A[r][:, :, None, :]), axis=1)
            near = (dd < TH + (last[q] & 15)) & (row >= p[r][:, None, :]); hit = np.any(near, axis=1)
            k = np.where(hit, 15 - np.argmax(near[:, ::-1], axis=1), p[r])
            hk = np.take_along_axis(h, k[:, None, :], 1)[:, 0]
            back = ((s[r] * hk >> 5) + s[r] + 811 * t) & (W - 1)
            new = np.where((row >= p[r][:, None, :]) & (row <= k[:, None, :]), back[:, None, :], P[r])
            turn = ~hit | (k == 15); tu = turn[:, None, :]
            for g in range(8):
                m = np.flatnonzero(~hit[g]); place, first = np.unique(hk[g][m], return_index=True); lane = m[first]
                X[q, g][:, place] = (X[q, g][:, place] + A[r, g][:, lane]) >> 1
            missed[q] = np.count_nonzero(~hit)
            P[r] = np.where(tu, new[:, ::-1], new); p[r] = np.where(turn, 15 - k, k + 1); s[r] = hk; ex[r] = ex[r] ^ turn
            A[r], R[r] = np.where(tu, R[r], A[r]), np.where(tu, A[r], R[r])
    at = [(q - (HO - 1)) % N for q in range(N)]
    return {"yn": P[at].reshape(N, 128, LN).astype(np.float32), "ys": s[at].astype(np.float32), "yp": (p[at] + 16 * ex[at]).astype(np.float32),
            "yx": X.reshape(N, 128, W).astype(np.float32).astype(BF)}

@@ -1,0 +1,475 @@
+import numpy as np
+from concourse.bass import DstId, RemoteDMATransfer
+from concourse.mybir import dt, AluOpType, AxisListType, ActivationFunctionType
+
+HO = 6
+F32, BF16, F16, I32, U16 = "float32", "bfloat16", "float16", "int32", "uint16"
+SCRATCH = {}
+for _n, _w, _d in (
+        ("X", 4352, BF16), ("DF", 4096, BF16), ("AB", 4096, BF16), ("EQ", 4096, F16),
+        ("EN", 2048, BF16), ("EF", 2048, F16), ("TR", 2048, F16), ("DK", 2048, F16), ("IJ", 2048, F16),
+        ("IM", 128, F16), ("IT", 128, F16), ("NI", 128, F16), ("IB", 128, BF16), ("NB", 128, BF16), ("B32", 128, F16),
+        ("BO", 128, F16), ("HF", 128, F16), ("BG", 128, BF16), ("BM", 128, F16),
+        ("IC", 256, I32), ("PI", 8, I32), ("PF", 16, F32), ("M16", 128, I32), ("MG", 256, I32), ("C1", 64, I32),
+        ("LL1", 34, U16), ("LL2", 18, U16), ("LB", 16, U16), ("LL3", 36, U16), ("LL3R", 32, U16), ("LL4", 18, U16),
+        ("CN", 256, BF16), ("C63", 64, BF16), ("MB", 64, BF16), ("NT", 272, I32), ("KAPI", 1, I32), ("KC", 8, F32),
+        ("KR", 32, F16), ("PX", 256, F16), ("AA", 256, BF16), ("RR", 256, BF16), ("RH", 256, BF16), ("AN", 256, BF16),
+        ("T1", 576, F32), ("T2", 576, F32), ("T3", 512, F32), ("T4", 512, F32), ("A2", 512, BF16),
+        ("PR", 256, F32), ("ZI", 256, I32), ("HI", 256, I32), ("HU", 256, U16), ("KN", 256, I32), ("UU", 256, I32),
+        ("TM", 256, F32), ("TX", 256, F32), ("SM", 256, F32), ("HKU", 16, U16), ("OU", 16, U16), ("BC", 16, F16),
+        ("MI", 16, F16), ("MK", 256, F32), ("TS", 256, F16), ("FS", 256, BF16), ("VS", 256, F32), ("VB", 256, BF16),
+        ("MC", 8, F32), ("MCI", 8, I32), ("LX", 288, F32), ("KX", 288, F32), ("NR", 256, F32), ("NH", 256, F32),
+        ("YO", 256, F32), ("SMF", 512, F32), ("SMI", 128, I32)):
+    SCRATCH[_n] = ("sbuf", [128, _w], _d)
+SMALL = {}
+for _i, _n in enumerate(("PE16", "PR16", "LT16", "KL", "KLR", "KD", "KE", "NDUM", "S32", "SF", "WB", "HP", "BP", "LIM", "KS", "KQ", "TU",
+                         "UN", "W1", "W2", "W3", "W4", "W5", "TQ", "TQ0", "O1", "O2", "O3", "NHK")):
+    SMALL[_n] = ("SMF", 16 * _i)
+for _i, _n in enumerate(("MM", "HK", "BZ", "BI", "DL")):
+    SMALL[_n] = ("SMI", 16 * _i)
+PSUM = ("Y0", "Y1", "ZP", "QP", "UP", "TP", "BPS", "FC")
+for _n in PSUM:
+    SCRATCH[_n] = ("psum", [128, 512], F32)
+for _t in range(HO):
+    SCRATCH["S%d" % _t] = ("sbuf", [128, 80], F16)
+    SCRATCH["P%d" % _t] = ("sbuf", [128, 256], F16)
+for _r in range(4):
+    SCRATCH["AR%d" % _r] = ("sbuf", [128, 512], BF16)
+for _t in range(2):
+    SCRATCH["SO%d" % _t] = ("sbuf", [128, 80], F16)
+    SCRATCH["PO%d" % _t] = ("sbuf", [128, 256], F16)
+SEMAPHORES = (["cV", "cA", "cT", "cG"] + ["d%d" % i for i in range(12)] + ["rS%d" % t for t in range(1, HO)] +
+              ["rP%d" % t for t in range(1, HO)] + ["rA%d" % r for r in range(4)] + ["lS%d" % t for t in range(1, HO)] +
+              ["lP%d" % t for t in range(1, HO)] + ["lA%d" % r for r in range(4)])
+
+
+def make_tracker(g, T):
+    queue = {"V": g.vector, "A": g.scalar, "T": g.tensor, "G": g, "S": g.sync}
+    count = {"V": 0, "A": 0, "T": 0, "G": 0}
+    know = {e: {} for e in queue}
+    snap = {}
+    hist = {}
+    allsem = {}
+
+    def ap(v):
+        if v[0] == "ind":
+            return ap(v[1]).indirect(ap(v[2]))
+        t = T[v[0]]
+        return t[:, v[1]:v[2]] if v[3] == 1 else t[:, v[1]:v[2]:v[3]]
+
+    def flat(vs):
+        out = []
+        for v in vs:
+            if isinstance(v, tuple):
+                out += [v[1], v[2]] if v[0] == "ind" else [v]
+        return out
+
+    def deps(eng, reads, writes):
+        need = {}
+        for is_w, vs in ((False, reads), (True, writes)):
+            for (b, lo, hi, st) in vs:
+                ps = b in PSUM
+                for (w, e, l2, h2, sem, val) in hist.get(b, ()):
+                    same = e == eng and eng in count
+                    if same or not ps:
+                        if not (w or is_w) or hi <= l2 or h2 <= lo:
+                            continue
+                        if same and (not w or (ps and eng == "T")):
+                            continue
+                    if need.get(sem, 0) < val:
+                        need[sem] = val
+        return need
+
+    def wait(eng, need):
+        kn = know[eng]
+        for sem in sorted(need, key=lambda s: (-len(snap.get((s, need[s]), ())), s)):
+            val = need[sem]
+            if kn.get(sem, 0) >= val:
+                continue
+            queue[eng].wait_ge(T.sem[sem], val)
+            kn[sem] = val
+            for s2, v2 in snap.get((sem, val), {}).items():
+                if kn.get(s2, 0) < v2:
+                    kn[s2] = v2
+
+    def note(eng, reads, writes, sem, val, kn):
+        for is_w, vs in ((True, writes), (False, reads)):
+            for (b, lo, hi, st) in vs:
+                h = hist.setdefault(b, [])
+                if eng != "dma":
+                    if is_w and st == 1 and b not in PSUM:
+                        h[:] = [x for x in h if not (lo <= x[2] and x[3] <= hi)]
+                    h[:] = [x for x in h if not (x[1] == eng and x[0] == is_w and x[2] == lo and x[3] == hi)]
+                h.append((is_w, eng, lo, hi, sem, val))
+        snap[(sem, val)] = dict(kn)
+        allsem[sem] = val
+
+    def op(eng, fn, reads, writes):
+        reads, writes = flat(reads), flat(writes)
+        wait(eng, deps(eng, reads, writes))
+        count[eng] += 1
+        fn(queue[eng]).then_inc(T.sem["c" + eng], 1)
+        note(eng, reads, writes, "c" + eng, count[eng], know[eng])
+
+    def dma(eng, sem, fn, reads, writes):
+        wait(eng, deps("dma", reads, writes))
+        fn(queue[eng]).then_inc(T.sem[sem], 16)
+        note("dma", reads, writes, sem, 16, know[eng])
+
+    def send(fn, reads, sem, val):
+        wait("G", deps("dma", reads, []))
+        fn(g)
+        note("dma", reads, [], sem, val, know["G"])
+
+    def arrival(v, sem, val):
+        note("dma", [], [v], sem, val, {})
+
+    def finish():
+        for sem in sorted(allsem):
+            wait("G", {sem: allsem[sem]})
+    return ap, op, dma, send, arrival, finish
+
+
+def rank_program(g, core, T, topo):
+    rank = T.rank_of(core)
+    if rank is None:
+        return
+    N = len(T.cores)
+    A = AluOpType
+    AF = ActivationFunctionType
+    ap, op, dma, send, arrival, finish = make_tracker(g, T)
+
+    def v(b, lo=0, hi=None, st=1):
+        if b in SMALL:
+            n, base = SMALL[b]
+            return (n, base + lo, base + (16 if hi is None else hi), st)
+        return (b, lo, SCRATCH[b][1][1] if hi is None else hi, st)
+
+    def ind(w, o):
+        return ("ind", w, o)
+
+    def sc_(x):
+        return ap(x) if isinstance(x, tuple) else x
+
+    def ts(out, in0, s1, op0, s2=None, op1=None):
+        if op1 is None:
+            op("V", lambda q: q.tensor_scalar(ap(out), ap(in0), sc_(s1), None, op0), [in0, s1], [out])
+        else:
+            op("V", lambda q: q.tensor_scalar(ap(out), ap(in0), sc_(s1), sc_(s2), op0, op1), [in0, s1, s2], [out])
+
+    def tt(out, in0, in1, o):
+        if out[0] == "ind":
+            op("V", lambda q: q.tensor_tensor(ap(out), ap(in0), ap(in1), o), [in0, in1, out[2]], [out[1]])
+        else:
+            op("V", lambda q: q.tensor_tensor(ap(out), ap(in0), ap(in1), o), [in0, in1], [out])
+
+    def cp(out, in_):
+        op("V", lambda q: q.tensor_copy(ap(out), ap(in_)), [in_], [out])
+
+    def fill(out, c):
+        op("V", lambda q: q.memset(ap(out), c), [], [out])
+
+    def act(out, in_, func, bias=0.0, scale=1.0):
+        op("A", lambda q: q.activation(ap(out), ap(in_), func, bias=sc_(bias), scale=sc_(scale)), [in_, bias, scale], [out])
+
+    def mm(out, l, r, start=True, stop=True):
+        op("T", lambda q: q.matmul(ap(out), ap(l), ap(r), start, stop), [l, r], [out])
+
+    def tp(out, in_):
+        op("V", lambda q: q.transpose(ap(out), ap(in_)), [in_], [out])
+
+    def iota(out, pattern, cm):
+        op("G", lambda q: q.iota(ap(out), pattern, 0, cm), [], [out])
+
+    def m128(b, j):
+        return v(b, 128 * j, 128 * j + 128)
+
+    def blk(b, j):
+        return v(b, 16 * j, 16 * j + 16)
+
+    def remote(dst, ob, ib, rsem, lsem):
+        rid, pid, _ = topo.addr(dst)
+        msk = topo.mask(core, dst)
+        send(lambda q: q.remote_dma(out_ap=T[ob][:], in_ap=T[ib][:], remote_sem=T.sem[rsem], local_sem=T.sem[lsem],
+                                    pid=pid, routing_id=rid, dma_engine_mask=msk), [v(ib)], lsem, len(topo.engines(core, dst)))
+
+    def incs(src, dst):
+        return len(topo.engines(src, dst))
+
+    nxt, prv = T.cores[(rank + 1) % N], T.cores[(rank - 1) % N]
+    for t in range(1, HO):
+        arrival(v("S%d" % t), "rS%d" % t, incs(prv, core))
+        arrival(v("P%d" % t), "rP%d" % t, incs(prv, core))
+    for r in range(N):
+        if r != rank:
+            arrival(v("AR%d" % r), "rA%d" % r, incs(T.cores[r], core))
+
+    dma("A", "d0", lambda q: q.dma_start(T.NT[:, 0:256], T.pn[:, :]), [], [v("NT", 0, 256)])
+    dma("S", "d1", lambda q: q.dma_start(T.NT[:, 256:272], T.s0[:, :]), [], [v("NT", 256, 272)])
+    dma("A", "d2", lambda q: q.dma_start(T.KAPI[:, :], T.kap[:, :]), [], [v("KAPI")])
+    dma("S", "d5", lambda q: q.dma_start(T.X[:, 0:4096], T.x[:, :]), [], [v("X", 0, 4096)])
+    dma("A", "d3", lambda q: q.dma_start(T.AA[:, :], T.a0[:, :]), [], [v("AA")])
+    dma("A", "d4", lambda q: q.dma_start(T.RR[:, :], T.r0[:, :]), [], [v("RR")])
+    me = "AR%d" % rank
+    act(v(me, 0, 256), v("AA"), AF.Copy)
+    act(v("AN"), v("AA"), AF.Copy, scale=-0.5)
+    act(v("RH"), v("RR"), AF.Copy, scale=0.5)
+
+    iota(v("IC"), [[1, 256]], 0)
+    iota(v("PI", 0, 1), [[1, 1]], 1)
+    pI = v("PI", 0, 1)
+    ts(v("PI", 1, 2), pI, 15, A.bitwise_and)
+    ts(v("PI", 2, 3), pI, 4, A.arith_shift_right)
+    ts(v("PI", 3, 4), pI, 4, A.arith_shift_right, 1, A.bitwise_and)
+    ts(v("C1"), v("IC", 0, 64), 1, A.arith_shift_right)
+    cp(v("PF", 0, 4), v("PI", 0, 4))
+    pf, p16, pg, hf = [v("PF", i, i + 1) for i in range(4)]
+    h16, x32, y32, k16, r16 = [v("PF", i, i + 1) for i in range(4, 9)]
+    ts(v("LL1"), v("C1", 0, 34), 16.0, A.mult, p16, A.add)
+    ts(h16, hf, 16.0, A.mult, p16, A.add)
+    ts(v("MG"), v("IC"), 4, A.arith_shift_right)
+    ts(x32, p16, 31.0, A.mult, h16, A.add)
+    ts(y32, h16, 512.0, A.add)
+    ts(v("IM"), v("IC", 0, 128), pf, A.is_equal)
+    ts(v("BO"), v("MG", 0, 128), pg, A.is_equal)
+    ts(v("LL2", 0, 16), v("IC", 0, 16), x32, A.add)
+    ts(v("LL2", 16, 17), v("IC", 0, 1), y32, A.add)
+    ts(v("LB"), v("IC", 0, 16), 0.0, A.mult, p16, A.add)
+    ts(v("IT"), v("IM"), 3232.0, A.mult)
+    ts(v("B32"), v("BO"), 32.0, A.mult)
+    cp(v("T1", 0, 544), ind(v("NT"), v("LL1")))
+    tp(v("T2", 0, 544), v("T1", 0, 544))
+    kc = [v("KC", i, i + 1) for i in range(3)]
+    cp(kc[0], v("KAPI"))
+    ts(kc[1], kc[0], 2048.0, A.is_ge, -4096.0, A.mult)
+    tt(kc[2], kc[0], kc[1], A.add)
+    ts(v("PX"), v("MG"), p16, A.is_equal, kc[2], A.mult)
+    ts(v("T3", 0, 272), ind(v("T2", 0, 544), v("LL2", 0, 17)), -2048.0, A.add)
+    cp(v("S0", 0, 16), v("T3", 256, 272))
+    cp(v("P0"), v("T3", 0, 256))
+    for lo, c in ((16, 0.0), (32, 4.0), (48, 2.0), (64, 0.0)):
+        ts(v("S0", lo, lo + 16), v("IC", 0, 16), 0.0, A.mult, c, A.add)
+    tt(v(me, 256, 512), v("RH"), v("AN"), A.add)
+    for d in range(1, N):
+        remote(T.cores[(rank + d) % N], me, me, "rA%d" % rank, "lA%d" % ((rank + d) % N))
+
+    def late_constants():
+        ts(v("M16"), v("IC", 0, 128), 15, A.bitwise_and)
+        fill(v("MB"), 63.5)
+        ts(v("IB"), v("IM"), 1.0, A.mult)
+        ts(v("NB"), v("IM"), -1.0, A.mult)
+        ts(v("M16"), v("M16"), 1.0, A.add)
+        ts(v("BG"), v("IM"), 524288.0, A.mult)
+        tt(v("BM"), v("BO"), v("M16"), A.mult)
+        ts(v("NI"), v("IM"), -1.0, A.mult)
+        for y in range(16):
+            ts(m128("EN", y), v("BM"), float(y + 1), A.is_equal, -524288.0, A.mult)
+        for j in range(1, 16):
+            ts(m128("IJ", j), v("IM"), 4096.0 * j, A.mult)
+        ts(v("PE16"), v("IC", 0, 16), p16, A.is_equal)
+        ts(v("LT16"), v("IC", 0, 16), p16, A.is_gt, -8192.0, A.mult)
+        for y in range(16):
+            ts(m128("EF", y), v("BO"), v("PE16", y, y + 1), A.mult)
+        for y in range(16):
+            ts(m128("TR", y), v("BM"), float(y + 1), A.is_equal, v("LT16", y, y + 1), A.mult)
+        fill(v("CN"), -192.0)
+        fill(v("C63"), 63.5)
+        ts(v("HF"), v("IM"), 0.0, A.mult, 0.5, A.add)
+        ts(v("NDUM"), v("IC", 0, 16), -16.0, A.mult, p16, A.subtract)
+        ts(v("NDUM"), v("NDUM"), -4096.0, A.add)
+        ts(r16, p16, -1.0, A.mult, 15.0, A.add)
+        ts(v("PR16"), v("IC", 0, 16), r16, A.is_equal)
+        ts(v("KR", 0, 16), v("PE16"), kc[2], A.mult)
+        ts(v("KR", 16, 32), v("PR16"), kc[2], A.mult)
+        mm(v("FC", 0, 32), v("BO"), v("KR"))
+        cp((SMALL["KL"][0], SMALL["KL"][1], SMALL["KL"][1] + 32, 1), v("FC", 0, 32))
+        tt(v("KD"), v("KLR"), v("KL"), A.subtract)
+        ts(v("KE"), v("KD"), 2048.0, A.is_ge, -4096.0, A.mult)
+        tt(v("KE"), v("KE"), v("KD"), A.add)
+        ts(v("KD"), v("KE"), -2048.0, A.is_lt, 4096.0, A.mult)
+        tt(v("KD"), v("KE"), v("KD"), A.add)
+        ts(v("KD"), v("KD"), 16.0, A.mult)
+        for j in range(16):
+            ts(m128("DK", j), v("IM"), v("KD", j, j + 1), A.mult)
+
+    def output_lists():
+        ts(k16, p16, 16.0, A.mult)
+        ts(r16, p16, -16.0, A.mult, 240.0, A.add)
+        ts(v("LL3", 0, 32), v("C1", 0, 32), k16, A.add)
+        ts(v("LL3", 32, 34), v("IC", 0, 2), 0.0, A.mult, p16, A.add)
+        ts(v("LL3", 32, 34), v("LL3", 32, 34), 256.0, A.add)
+        ts(v("LL3", 34, 36), v("LL3", 32, 34), 16.0, A.add)
+        ts(v("LL3R"), v("C1", 0, 32), r16, A.add)
+        ts(v("LL4"), v("IC", 0, 18), 32.0, A.mult, h16, A.add)
+
+    def spread(out, src):
+        for y in range(16):
+            mm((out, y, 256, 16), m128("EF", y), src)
+
+    for t in range(HO):
+        last = t == HO - 1
+        S, P = "S%d" % t, "P%d" % t
+        sc, u2, e4, w4, pp = [v(S, 16 * i, 16 * i + 16) for i in range(5)]
+        ar = "AR%d" % ((rank - t) % N)
+        so, po = "SO%d" % (t % 2), "PO%d" % (t % 2)
+        if t:
+            spread("UP", u2)
+        mm(v("ZP", 0, 256), v("B32"), v("PX"), True, False)
+        for j in range(16):
+            mm(blk("ZP", j), v("IT"), sc, False, t == 0 and j == 15)
+            if t:
+                mm(blk("ZP", j), m128("DK", j), u2, False, j == 15)
+        ts(v("S32"), sc, 2080.0, A.add)
+        if t:
+            tt(v("UP", 256, 512), v("UP", 0, 256), v(ar, 256, 512), A.mult)
+            ts(v("SF"), sc, 2048.0, A.add)
+            tt(v("A2", 0, 256), v("UP", 256, 512), v(ar, 0, 256), A.add)
+        else:
+            cp(v("A2", 0, 256), v(ar, 0, 256))
+            ts(v("SF"), sc, 2048.0, A.add)
+        tt(v("PR"), ind(v("S32"), v("LB")), v(P), A.mult)
+        cp(v("A2", 256, 512), v("A2", 0, 256))
+        tt(v("ZI"), v("PR"), v("ZP", 0, 256), A.add)
+        ts(v("WB"), v("SF"), 32.0, A.mult, float((25952 * t) % 131072 - 262144), A.add)
+        ts(v("HI"), v("ZI"), 5, A.arith_shift_right, 4095, A.bitwise_and)
+        cp(v("HU"), v("HI"))
+        if t == 0:
+            late_constants()
+        for j in range(16):
+            if j:
+                mm(blk("QP", j), m128("IJ", j), e4, True, False)
+            mm(blk("QP", j), m128("IJ", 1), w4, j == 0, True)
+        act(v("DF", 3584, 4096), ind(v("X", 0, 4096), v("HU", 224, 256)), AF.Copy)
+        mm(v("FC"), v("IB"), v("DF", 3584, 4096), True, False)
+        mm(v("FC"), v("NB"), v("A2"), False, True)
+        for i in range(7):
+            sl = (512 * i, 512 * i + 512)
+            tt(v("DF", *sl), ind(v("X", 0, 4096), v("HU", 32 * i, 32 * i + 32)), v("A2"), A.subtract)
+            act(v("AB", *sl), v("DF", *sl), AF.Abs)
+            if i == 0:
+                act(v("AB", 3584, 4096), v("FC"), AF.Abs)
+            if i % 2 or i == 6:
+                c = i // 2
+                o = v("Y0", 64 * c, 64 * c + 64) if c < 3 else v("Y1", 0, 64)
+                mm(o, v("BG"), v("MB"), True, False)
+                for y in range(16):
+                    mm(o, m128("EN", y), ("AB", 1024 * c + y, 1024 * c + 1024, 16), False, y == 15)
+        mm(v("BPS", 0, 256), v("NI"), v(P), True, False)
+        tt(v("KN"), v("QP", 0, 256), v("HI"), A.add)
+        ts(v("UU"), v("KN"), 0xFFFFFF, A.bitwise_and)
+        tt(v("SM", 0, 192), v("KN", 0, 192), v("Y0", 0, 192), A.min)
+        tt(v("TM", 0, 128), v("UU", 0, 128), v("UU", 128, 256), A.min)
+        tt(v("TX", 0, 96), v("SM", 0, 96), v("SM", 96, 192), A.max)
+        tt(v("TM", 128, 192), v("TM", 0, 64), v("TM", 64, 128), A.min)
+        tt(v("TX", 96, 144), v("TX", 0, 48), v("TX", 48, 96), A.max)
+        tt(v("TM", 192, 224), v("TM", 128, 160), v("TM", 160, 192), A.min)
+        tt(v("TX", 144, 160), v("TX", 96, 112), v("TX", 112, 128), A.max)
+        tt(v("TM", 224, 240), v("TM", 192, 208), v("TM", 208, 224), A.min)
+        tt(v("TX", 160, 176), v("TX", 128, 144), v("TX", 144, 160), A.max)
+        ts(v("HP"), v("TM", 224, 240), -8192.0, A.add)
+        tt(v("SM", 192, 256), v("KN", 192, 256), v("Y1", 0, 64), A.min)
+        tt(v("TX", 176, 192), v("TX", 160, 176), v("HP"), A.max)
+        tt(v("TX", 192, 224), v("SM", 192, 224), v("SM", 224, 256), A.max)
+        tt(v("TX", 224, 240), v("TX", 192, 208), v("TX", 176, 192), A.max)
+        tt(v("MM"), v("TX", 208, 224), v("TX", 224, 240), A.max)
+        nsc, nu2, ne4, nw4, npp = [v(so, 16 * i, 16 * i + 16) for i in range(5)]
+        ts(v("HK"), v("MM"), 4095, A.bitwise_and)
+        ts(v("DL"), v("MM"), 14, A.arith_shift_right)
+        ts(v("MI"), v("MM"), 8192.0, A.is_lt, 2.0, A.mult)
+        tt(v("BP"), v("SF"), v("HK"), A.mult)
+        ts(nsc, v("HK"), -2048.0, A.add)
+        spread("TP", nsc)
+        tt(v("KS"), pp, v("DL"), A.add)
+        tt(v("BZ"), v("BP"), v("WB"), A.add)
+        ts(v("LIM"), v("DL"), 16384.0, A.mult, 16383.0, A.add)
+        ts(v("KQ"), v("KS"), 15.0, A.is_equal, 2.0, A.mult)
+        ts(v("BI"), v("BZ"), 5, A.arith_shift_right, 4095, A.bitwise_and)
+        ts(v("W1"), v("KS"), -1.0, A.mult, 7.0, A.add)
+        tt(v("TU"), v("KQ"), v("MI"), A.max)
+        ts(v("BC"), v("BI"), -2048.0, A.add)
+        for j in range(16):
+            mm(blk("BPS", j), v("IM"), v("BC"), False, j == 15)
+        ts(v("W3"), v("KS"), 1.0, A.add)
+        tt(v("UN"), u2, v("TU"), A.not_equal)
+        tt(v("W2"), v("W1"), v("TU"), A.mult)
+        ts(v("TQ0"), v("MM"), 8192.0, A.is_ge, -12000.0, A.mult)
+        ts(nu2, v("UN"), 2.0, A.mult)
+        tt(npp, v("W2"), v("W3"), A.add)
+        if not last:
+            ts(v("W4"), v("UN"), 15.0, A.mult)
+            ts(ne4, v("UN"), -8.0, A.mult, 4.0, A.add)
+            tt(v("W5"), v("W4"), npp, A.subtract)
+            tt(v("TQ"), v("TQ0"), nsc, A.add)
+            ts(nw4, v("W5"), 4.0, A.mult, 2.0, A.add)
+            remote(nxt, "S%d" % (t + 1), so, "rS%d" % (t + 1), "lS%d" % (t + 1))
+            mm(v("Y0", 256, 272), v("HF"), v("MI"))
+        else:
+            tt(v("TQ"), v("TQ0"), nsc, A.add)
+
+        def names():
+            tt(v("BPS", 256, 512), v("BPS", 0, 256), v("MK"), A.mult)
+            tt(v(po), v("BPS", 256, 512), v(P), A.add)
+
+        def compare(bs):
+            for b in bs:
+                ts(v("EQ", 272 * b, 256 * b + 256), v("TS", 16 * b, 256), v("TQ", b, b + 1), A.is_equal)
+                if b < 15:
+                    mm(v("FC", 16 * b + 16, 256), v("BO"), v("EQ", 272 * b + 16, 256 * b + 256), b == 0, b == 14)
+
+        cp(v("TS"), v("TP", 0, 256))
+        tt(v("MK"), ind(v("LIM"), v("LB")), v("UU"), A.is_ge)
+        if last:
+            compare(range(16))
+        else:
+            compare(range(0, 3))
+            names()
+            remote(nxt, "P%d" % (t + 1), po, "rP%d" % (t + 1), "lP%d" % (t + 1))
+            compare(range(3, 16))
+        cp(v("HKU"), v("HK"))
+        act(v("FS", 16, 256), v("FC", 16, 256), AF.Copy)
+        if t == 0:
+            fill(v("FS", 0, 16), 0.0)
+        for y in range(16):
+            mm(v("Y1", 256, 272), m128("TR", y), ("EQ", y, y + 4081, 272), y == 0, False)
+        for y in range(16):
+            mm(v("Y1", 256, 272), m128("EN", y), ("FS", y, 256, 16), False, y == 15)
+        tt(v("O1"), v("TQ0"), v("NDUM"), A.max)
+        ts(v("NHK"), v("HK"), -1.0, A.mult)
+        tt(v("VS"), ind(v("X", 0, 4096), v("HKU")), v("A2", 0, 256), A.add)
+        act(v("VB"), v("VS"), AF.Copy, bias=191.75, scale=0.5)
+        if not last:
+            op("V", lambda q: q.tensor_reduce(T.MC[:, 0:1], T.Y0[:, 256:272], AxisListType.X, A.add), [v("Y0", 256, 272)], [v("MC", 0, 1)])
+            tt(v("O1"), v("O1"), v("NHK"), A.min)
+            cp(v("MCI", 0, 1), v("MC", 0, 1))
+            ts(v("MCI", 1, 2), v("MCI", 0, 1), 15, A.bitwise_and)
+            cp(v("MC", 1, 2), v("MCI", 1, 2))
+            act(v("MB"), v("C63"), AF.Identity, bias=v("MC", 1, 2))
+        else:
+            tt(v("O1"), v("O1"), v("NHK"), A.min)
+            output_lists()
+        tt(v("O2"), v("Y1", 256, 272), v("NDUM"), A.max)
+        tt(v("O3"), v("O2"), v("O1"), A.min)
+        ts(v("OU"), v("O3"), -1.0, A.mult)
+        tt(ind(v("X"), v("OU")), v("VB"), v("CN"), A.add)
+        if last:
+            dma("S", "d6", lambda q: q.dma_start(T.yx[:, :], T.X[:, 0:4096]), [v("X", 0, 4096)], [])
+            spread("UP", nu2)
+            names()
+            ts(v("W1"), nu2, 8.0, A.mult)
+            ts(v("LX", 0, 256), v(po), 2048.0, A.add)
+            cp(v("LX", 256, 272), v("HK"))
+            tt(v("LX", 272, 288), v("W1"), npp, A.add)
+            cp(v("T3"), ind(v("LX", 0, 256), v("LL3R")))
+            cp(v("T1"), ind(v("LX"), v("LL3")))
+            tp(v("T4"), v("T3"))
+            tp(v("T2"), v("T1"))
+            ts(v("NR"), ind(v("T4"), v("LL4", 0, 16)), 0.5, A.mult)
+            cp(v("KX"), ind(v("T2"), v("LL4")))
+            dma("A", "d7", lambda q: q.dma_start(T.ys[:, :], T.KX[:, 256:272]), [v("KX", 256, 272)], [])
+            dma("S", "d8", lambda q: q.dma_start(T.yp[:, :], T.KX[:, 272:288]), [v("KX", 272, 288)], [])
+            ts(v("NH"), v("KX", 0, 256), 0.5, A.mult)
+            tt(v("NH"), v("NR"), v("NH"), A.subtract)
+            tt(v("UP", 256, 512), v("UP", 0, 256), v("NH"), A.mult)
+            tt(v("YO"), v("UP", 256, 512), v("KX", 0, 256), A.add)
+            dma("A", "d9", lambda q: q.dma_start(T.yn[:, :], T.YO[:, :]), [v("YO")], [])
+    finish()

@@ -7,22 +7,21 @@ F32, BF16, F16, I32, U16 = "float32", "bfloat16", "float16", "int32", "uint16"
 SCRATCH = {}
 for _n, _w, _d in (
         ("X", 4352, BF16), ("DF", 4096, BF16), ("AB", 4096, BF16), ("EQ", 4096, F16),
-        ("EN", 2048, BF16), ("EF", 2048, F16), ("TR", 2048, F16), ("DK", 2048, F16), ("IJ", 2048, F16),
-        ("IM", 128, F16), ("IT", 128, F16), ("NI", 128, F16), ("IB", 128, BF16), ("NB", 128, BF16), ("B32", 128, F16),
-        ("BO", 128, F16), ("HF", 128, F16), ("BG", 128, BF16), ("BM", 128, F16),
-        ("IC", 256, I32), ("PI", 8, I32), ("PF", 16, F32), ("M16", 128, I32), ("MG", 256, I32), ("C1", 64, I32),
-        ("LL1", 34, U16), ("LL2", 18, U16), ("LB", 16, U16), ("LL3", 36, U16), ("LL3R", 32, U16), ("LL4", 18, U16),
+        ("EN", 2048, BF16), ("EF", 2048, BF16), ("TR", 2048, BF16), ("DK", 2048, F16), ("IJ", 2048, BF16),
+        ("IT", 128, BF16), ("IB", 128, BF16), ("NB", 128, BF16), ("B32", 128, BF16),
+        ("BO", 128, BF16), ("BOS", 128, BF16), ("HF", 128, BF16), ("BG", 128, BF16), ("LREV", 16, U16),
+        ("IC", 256, I32), ("PI", 8, I32), ("PF", 16, F32), ("MG", 256, I32), ("C1", 64, I32),
+        ("LL1", 34, U16), ("LL2", 18, U16), ("LB", 16, U16), ("LL3", 36, U16), ("LL4", 18, U16), ("HPC", 16, F16),
         ("CN", 256, BF16), ("C63", 64, BF16), ("MB", 64, BF16), ("NT", 272, I32), ("KAPI", 1, I32), ("KC", 8, F32),
         ("KR", 32, F16), ("PX", 256, F16), ("AA", 256, BF16), ("RR", 256, BF16), ("RH", 256, BF16), ("AN", 256, BF16),
-        ("T1", 576, F32), ("T2", 576, F32), ("T3", 512, F32), ("T4", 512, F32), ("A2", 512, BF16),
+        ("T1", 576, F32), ("T2", 576, F32), ("T3", 288, F32), ("A2", 512, BF16),
         ("PR", 256, F32), ("ZI", 256, I32), ("HI", 256, I32), ("HU", 256, U16), ("KN", 256, I32), ("UU", 256, I32),
         ("TM", 256, F32), ("TX", 256, F32), ("SM", 256, F32), ("HKU", 16, U16), ("OU", 16, U16), ("BC", 16, F16),
         ("MI", 16, F16), ("MK", 256, F32), ("TS", 256, F16), ("FS", 256, BF16), ("VS", 256, F32), ("VB", 256, BF16),
-        ("MC", 8, F32), ("MCI", 8, I32), ("LX", 288, F32), ("KX", 288, F32), ("NR", 256, F32), ("NH", 256, F32),
-        ("YO", 256, F32), ("SMF", 512, F32), ("SMI", 128, I32)):
+        ("MC", 8, F32), ("MCI", 8, I32), ("LX", 288, F32), ("KX", 288, F32), ("LP", 256, F32), ("SMF", 512, F32), ("SMI", 128, I32)):
     SCRATCH[_n] = ("sbuf", [128, _w], _d)
 SMALL = {}
-for _i, _n in enumerate(("PE16", "PR16", "LT16", "KL", "KLR", "KD", "KE", "NDUM", "S32", "SF", "WB", "HP", "BP", "LIM", "KS", "KQ", "TU",
+for _i, _n in enumerate(("PE16", "PEN", "PR16", "LT16", "KL", "KLR", "KD", "KE", "NDUM", "S32", "SF", "WB", "HP", "BP", "LIM", "KS", "KQ", "TU",
                          "UN", "W1", "W2", "W3", "W4", "W5", "TQ", "TQ0", "O1", "O2", "O3", "NHK")):
     SMALL[_n] = ("SMF", 16 * _i)
 for _i, _n in enumerate(("MM", "HK", "BZ", "BI", "DL")):
@@ -211,9 +210,6 @@ def rank_program(g, core, T, topo):
     dma("A", "d3", lambda q: q.dma_start(T.AA[:, :], T.a0[:, :]), [], [v("AA")])
     dma("A", "d4", lambda q: q.dma_start(T.RR[:, :], T.r0[:, :]), [], [v("RR")])
     me = "AR%d" % rank
-    act(v(me, 0, 256), v("AA"), AF.Copy)
-    act(v("AN"), v("AA"), AF.Copy, scale=-0.5)
-    act(v("RH"), v("RR"), AF.Copy, scale=0.5)
 
     iota(v("IC"), [[1, 256]], 0)
     iota(v("PI", 0, 1), [[1, 1]], 1)
@@ -226,17 +222,32 @@ def rank_program(g, core, T, topo):
     pf, p16, pg, hf = [v("PF", i, i + 1) for i in range(4)]
     h16, x32, y32, k16, r16 = [v("PF", i, i + 1) for i in range(4, 9)]
     ts(v("LL1"), v("C1", 0, 34), 16.0, A.mult, p16, A.add)
-    ts(h16, hf, 16.0, A.mult, p16, A.add)
     ts(v("MG"), v("IC"), 4, A.arith_shift_right)
+    ts(h16, hf, 16.0, A.mult, p16, A.add)
+    ts(v("IB"), v("IC", 0, 128), pf, A.is_equal)
+    ts(v("BOS"), v("MG", 0, 128), pg, A.is_equal, -524288.0, A.mult)
+    ts(v("PE16"), v("IC", 0, 16), p16, A.is_equal)
     ts(x32, p16, 31.0, A.mult, h16, A.add)
     ts(y32, h16, 512.0, A.add)
-    ts(v("IM"), v("IC", 0, 128), pf, A.is_equal)
-    ts(v("BO"), v("MG", 0, 128), pg, A.is_equal)
+    ts(v("PEN"), v("PE16"), -1.0 / 524288.0, A.mult)
     ts(v("LL2", 0, 16), v("IC", 0, 16), x32, A.add)
     ts(v("LL2", 16, 17), v("IC", 0, 1), y32, A.add)
     ts(v("LB"), v("IC", 0, 16), 0.0, A.mult, p16, A.add)
-    ts(v("IT"), v("IM"), 3232.0, A.mult)
-    ts(v("B32"), v("BO"), 32.0, A.mult)
+    for y in range(16):
+        op("G", lambda q, y=y: q.affine_select(ap(m128("EN", y)), ap(v("BOS")), [[0, 8], [1, 16]], A.is_equal, 0.0, -y, 0),
+           [v("BOS")], [m128("EN", y)])
+    act(v("B32"), v("BOS"), AF.Copy, scale=-32.0 / 524288.0)
+    act(v("IT"), v("IB"), AF.Copy, scale=3232.0)
+    act(v("NB"), v("IB"), AF.Copy, scale=-1.0)
+    act(v("BG"), v("IB"), AF.Copy, scale=524288.0)
+    act(v(me, 0, 256), v("AA"), AF.Copy)
+    act(v("AN"), v("AA"), AF.Copy, scale=-0.5)
+    act(v("RH"), v("RR"), AF.Copy, scale=0.5)
+    act(v("BO"), v("BOS"), AF.Copy, scale=-1.0 / 524288.0)
+    for j in range(1, 16):
+        act(m128("IJ", j), v("IB"), AF.Copy, scale=4096.0 * j)
+    for y in range(16):
+        act(m128("EF", y), v("BOS"), AF.Copy, scale=v("PEN", y, y + 1))
     cp(v("T1", 0, 544), ind(v("NT"), v("LL1")))
     tp(v("T2", 0, 544), v("T1", 0, 544))
     kc = [v("KC", i, i + 1) for i in range(3)]
@@ -254,35 +265,21 @@ def rank_program(g, core, T, topo):
         remote(T.cores[(rank + d) % N], me, me, "rA%d" % rank, "lA%d" % ((rank + d) % N))
 
     def late_constants():
-        ts(v("M16"), v("IC", 0, 128), 15, A.bitwise_and)
         fill(v("MB"), 63.5)
-        ts(v("IB"), v("IM"), 1.0, A.mult)
-        ts(v("NB"), v("IM"), -1.0, A.mult)
-        ts(v("M16"), v("M16"), 1.0, A.add)
-        ts(v("BG"), v("IM"), 524288.0, A.mult)
-        tt(v("BM"), v("BO"), v("M16"), A.mult)
-        ts(v("NI"), v("IM"), -1.0, A.mult)
-        for y in range(16):
-            ts(m128("EN", y), v("BM"), float(y + 1), A.is_equal, -524288.0, A.mult)
-        for j in range(1, 16):
-            ts(m128("IJ", j), v("IM"), 4096.0 * j, A.mult)
-        ts(v("PE16"), v("IC", 0, 16), p16, A.is_equal)
-        ts(v("LT16"), v("IC", 0, 16), p16, A.is_gt, -8192.0, A.mult)
-        for y in range(16):
-            ts(m128("EF", y), v("BO"), v("PE16", y, y + 1), A.mult)
-        for y in range(16):
-            ts(m128("TR", y), v("BM"), float(y + 1), A.is_equal, v("LT16", y, y + 1), A.mult)
-        fill(v("CN"), -192.0)
-        fill(v("C63"), 63.5)
-        ts(v("HF"), v("IM"), 0.0, A.mult, 0.5, A.add)
-        ts(v("NDUM"), v("IC", 0, 16), -16.0, A.mult, p16, A.subtract)
-        ts(v("NDUM"), v("NDUM"), -4096.0, A.add)
+        fill(v("HF"), 0.5)
         ts(r16, p16, -1.0, A.mult, 15.0, A.add)
-        ts(v("PR16"), v("IC", 0, 16), r16, A.is_equal)
         ts(v("KR", 0, 16), v("PE16"), kc[2], A.mult)
+        ts(v("PR16"), v("IC", 0, 16), r16, A.is_equal)
         ts(v("KR", 16, 32), v("PR16"), kc[2], A.mult)
-        mm(v("FC", 0, 32), v("BO"), v("KR"))
-        cp((SMALL["KL"][0], SMALL["KL"][1], SMALL["KL"][1] + 32, 1), v("FC", 0, 32))
+        mm(v("UP", 0, 32), v("BO"), v("KR"))
+        ts(v("LT16"), v("IC", 0, 16), p16, A.is_gt)
+        fill(v("CN"), -192.0)
+        ts(v("NDUM"), v("IC", 0, 16), -16.0, A.mult, p16, A.subtract)
+        fill(v("C63"), 63.5)
+        ts(v("NDUM"), v("NDUM"), -4096.0, A.add)
+
+    def key_matrices():
+        cp((SMALL["KL"][0], SMALL["KL"][1], SMALL["KL"][1] + 32, 1), v("UP", 0, 32))
         tt(v("KD"), v("KLR"), v("KL"), A.subtract)
         ts(v("KE"), v("KD"), 2048.0, A.is_ge, -4096.0, A.mult)
         tt(v("KE"), v("KE"), v("KD"), A.add)
@@ -290,16 +287,16 @@ def rank_program(g, core, T, topo):
         tt(v("KD"), v("KE"), v("KD"), A.add)
         ts(v("KD"), v("KD"), 16.0, A.mult)
         for j in range(16):
-            ts(m128("DK", j), v("IM"), v("KD", j, j + 1), A.mult)
+            ts(m128("DK", j), v("IB"), v("KD", j, j + 1), A.mult)
 
     def output_lists():
         ts(k16, p16, 16.0, A.mult)
-        ts(r16, p16, -16.0, A.mult, 240.0, A.add)
+        ts(r16, p16, 240.0, A.add)
+        ts(v("LREV"), v("IC", 0, 16), -16.0, A.mult, r16, A.add)
         ts(v("LL3", 0, 32), v("C1", 0, 32), k16, A.add)
         ts(v("LL3", 32, 34), v("IC", 0, 2), 0.0, A.mult, p16, A.add)
         ts(v("LL3", 32, 34), v("LL3", 32, 34), 256.0, A.add)
         ts(v("LL3", 34, 36), v("LL3", 32, 34), 16.0, A.add)
-        ts(v("LL3R"), v("C1", 0, 32), r16, A.add)
         ts(v("LL4"), v("IC", 0, 18), 32.0, A.mult, h16, A.add)
 
     def spread(out, src):
@@ -312,61 +309,69 @@ def rank_program(g, core, T, topo):
         sc, u2, e4, w4, pp = [v(S, 16 * i, 16 * i + 16) for i in range(5)]
         ar = "AR%d" % ((rank - t) % N)
         so, po = "SO%d" % (t % 2), "PO%d" % (t % 2)
-        if t:
-            spread("UP", u2)
         mm(v("ZP", 0, 256), v("B32"), v("PX"), True, False)
         for j in range(16):
             mm(blk("ZP", j), v("IT"), sc, False, t == 0 and j == 15)
             if t:
                 mm(blk("ZP", j), m128("DK", j), u2, False, j == 15)
+        if t:
+            spread("UP", u2)
         ts(v("S32"), sc, 2080.0, A.add)
+        ts(v("SF"), sc, 2048.0, A.add)
+        tt(v("PR"), ind(v("S32"), v("LB")), v(P), A.mult)
+        ts(v("WB"), v("SF"), 32.0, A.mult, float((25952 * t) % 131072 - 262144), A.add)
+        tt(v("ZI"), v("PR"), v("ZP", 0, 256), A.add)
+        if t == 0:
+            cp(v("A2", 0, 256), v(ar, 0, 256))
+        ts(v("HI"), v("ZI"), 5, A.arith_shift_right, 4095, A.bitwise_and)
         if t:
             tt(v("UP", 256, 512), v("UP", 0, 256), v(ar, 256, 512), A.mult)
-            ts(v("SF"), sc, 2048.0, A.add)
-            tt(v("A2", 0, 256), v("UP", 256, 512), v(ar, 0, 256), A.add)
-        else:
-            cp(v("A2", 0, 256), v(ar, 0, 256))
-            ts(v("SF"), sc, 2048.0, A.add)
-        tt(v("PR"), ind(v("S32"), v("LB")), v(P), A.mult)
-        cp(v("A2", 256, 512), v("A2", 0, 256))
-        tt(v("ZI"), v("PR"), v("ZP", 0, 256), A.add)
-        ts(v("WB"), v("SF"), 32.0, A.mult, float((25952 * t) % 131072 - 262144), A.add)
-        ts(v("HI"), v("ZI"), 5, A.arith_shift_right, 4095, A.bitwise_and)
         cp(v("HU"), v("HI"))
+        if t:
+            tt(v("A2", 0, 256), v("UP", 256, 512), v(ar, 0, 256), A.add)
+        cp(v("A2", 256, 512), v("A2", 0, 256))
         if t == 0:
             late_constants()
         for j in range(16):
             if j:
                 mm(blk("QP", j), m128("IJ", j), e4, True, False)
             mm(blk("QP", j), m128("IJ", 1), w4, j == 0, True)
-        act(v("DF", 3584, 4096), ind(v("X", 0, 4096), v("HU", 224, 256)), AF.Copy)
-        mm(v("FC"), v("IB"), v("DF", 3584, 4096), True, False)
+        act(v("DF", 0, 768), ind(v("X", 0, 4096), v("HU", 0, 48)), AF.Copy)
+        mm(v("FC"), v("IB"), v("DF", 0, 512), True, False)
         mm(v("FC"), v("NB"), v("A2"), False, True)
-        for i in range(7):
-            sl = (512 * i, 512 * i + 512)
-            tt(v("DF", *sl), ind(v("X", 0, 4096), v("HU", 32 * i, 32 * i + 32)), v("A2"), A.subtract)
+        mm(v("TP", 0, 256), v("IB"), v("DF", 512, 768), True, False)
+        mm(v("TP", 0, 256), v("NB"), v("A2", 0, 256), False, True)
+        for i in range(1, 8):
+            sl = (512 * i, 512 * i + 512) if i > 1 else (768, 1024)
+            tt(v("DF", *sl), ind(v("X", 0, 4096), v("HU", sl[0] // 16, sl[1] // 16)), v("A2", 0, sl[1] - sl[0]), A.subtract)
             act(v("AB", *sl), v("DF", *sl), AF.Abs)
-            if i == 0:
-                act(v("AB", 3584, 4096), v("FC"), AF.Abs)
-            if i % 2 or i == 6:
-                c = i // 2
+            if i == 2:
+                act(v("AB", 0, 512), v("FC"), AF.Abs)
+                act(v("AB", 512, 768), v("TP", 0, 256), AF.Abs)
+            if i in (2, 3, 5, 7):
+                c = i // 2 if i != 2 else 0
                 o = v("Y0", 64 * c, 64 * c + 64) if c < 3 else v("Y1", 0, 64)
                 mm(o, v("BG"), v("MB"), True, False)
                 for y in range(16):
                     mm(o, m128("EN", y), ("AB", 1024 * c + y, 1024 * c + 1024, 16), False, y == 15)
-        mm(v("BPS", 0, 256), v("NI"), v(P), True, False)
+        mm(v("BPS", 0, 256), v("NB"), v(P), True, False)
+        if t == 0:
+            for y in range(16):
+                act(m128("TR", y), m128("EN", y), AF.Copy, scale=v("LT16", y, y + 1))
         tt(v("KN"), v("QP", 0, 256), v("HI"), A.add)
         ts(v("UU"), v("KN"), 0xFFFFFF, A.bitwise_and)
-        tt(v("SM", 0, 192), v("KN", 0, 192), v("Y0", 0, 192), A.min)
         tt(v("TM", 0, 128), v("UU", 0, 128), v("UU", 128, 256), A.min)
-        tt(v("TX", 0, 96), v("SM", 0, 96), v("SM", 96, 192), A.max)
         tt(v("TM", 128, 192), v("TM", 0, 64), v("TM", 64, 128), A.min)
-        tt(v("TX", 96, 144), v("TX", 0, 48), v("TX", 48, 96), A.max)
+        tt(v("SM", 0, 192), v("KN", 0, 192), v("Y0", 0, 192), A.min)
         tt(v("TM", 192, 224), v("TM", 128, 160), v("TM", 160, 192), A.min)
-        tt(v("TX", 144, 160), v("TX", 96, 112), v("TX", 112, 128), A.max)
+        tt(v("TX", 0, 96), v("SM", 0, 96), v("SM", 96, 192), A.max)
         tt(v("TM", 224, 240), v("TM", 192, 208), v("TM", 208, 224), A.min)
-        tt(v("TX", 160, 176), v("TX", 128, 144), v("TX", 144, 160), A.max)
+        tt(v("TX", 96, 144), v("TX", 0, 48), v("TX", 48, 96), A.max)
+        ts(v("HPC"), v("TM", 224, 240), -10240.0, A.add)
+        spread("TP", v("HPC"))
+        tt(v("TX", 144, 160), v("TX", 96, 112), v("TX", 112, 128), A.max)
         ts(v("HP"), v("TM", 224, 240), -8192.0, A.add)
+        tt(v("TX", 160, 176), v("TX", 128, 144), v("TX", 144, 160), A.max)
         tt(v("SM", 192, 256), v("KN", 192, 256), v("Y1", 0, 64), A.min)
         tt(v("TX", 176, 192), v("TX", 160, 176), v("HP"), A.max)
         tt(v("TX", 192, 224), v("SM", 192, 224), v("SM", 224, 256), A.max)
@@ -378,7 +383,6 @@ def rank_program(g, core, T, topo):
         ts(v("MI"), v("MM"), 8192.0, A.is_lt, 2.0, A.mult)
         tt(v("BP"), v("SF"), v("HK"), A.mult)
         ts(nsc, v("HK"), -2048.0, A.add)
-        spread("TP", nsc)
         tt(v("KS"), pp, v("DL"), A.add)
         tt(v("BZ"), v("BP"), v("WB"), A.add)
         ts(v("LIM"), v("DL"), 16384.0, A.mult, 16383.0, A.add)
@@ -388,7 +392,7 @@ def rank_program(g, core, T, topo):
         tt(v("TU"), v("KQ"), v("MI"), A.max)
         ts(v("BC"), v("BI"), -2048.0, A.add)
         for j in range(16):
-            mm(blk("BPS", j), v("IM"), v("BC"), False, j == 15)
+            mm(blk("BPS", j), v("IB"), v("BC"), False, j == 15)
         ts(v("W3"), v("KS"), 1.0, A.add)
         tt(v("UN"), u2, v("TU"), A.not_equal)
         tt(v("W2"), v("W1"), v("TU"), A.mult)
@@ -399,14 +403,15 @@ def rank_program(g, core, T, topo):
             ts(v("W4"), v("UN"), 15.0, A.mult)
             ts(ne4, v("UN"), -8.0, A.mult, 4.0, A.add)
             tt(v("W5"), v("W4"), npp, A.subtract)
-            tt(v("TQ"), v("TQ0"), nsc, A.add)
+            tt(v("TQ"), v("TQ0"), v("HPC"), A.add)
             ts(nw4, v("W5"), 4.0, A.mult, 2.0, A.add)
             remote(nxt, "S%d" % (t + 1), so, "rS%d" % (t + 1), "lS%d" % (t + 1))
             mm(v("Y0", 256, 272), v("HF"), v("MI"))
         else:
-            tt(v("TQ"), v("TQ0"), nsc, A.add)
+            tt(v("TQ"), v("TQ0"), v("HPC"), A.add)
 
         def names():
+            tt(v("MK"), ind(v("LIM"), v("LB")), v("UU"), A.is_ge)
             tt(v("BPS", 256, 512), v("BPS", 0, 256), v("MK"), A.mult)
             tt(v(po), v("BPS", 256, 512), v(P), A.add)
 
@@ -417,15 +422,13 @@ def rank_program(g, core, T, topo):
                     mm(v("FC", 16 * b + 16, 256), v("BO"), v("EQ", 272 * b + 16, 256 * b + 256), b == 0, b == 14)
 
         cp(v("TS"), v("TP", 0, 256))
-        tt(v("MK"), ind(v("LIM"), v("LB")), v("UU"), A.is_ge)
         if last:
             compare(range(16))
         else:
-            compare(range(0, 3))
             names()
             remote(nxt, "P%d" % (t + 1), po, "rP%d" % (t + 1), "lP%d" % (t + 1))
-            compare(range(3, 16))
-        cp(v("HKU"), v("HK"))
+            compare(range(16))
+        cp(v("HKU"), v("HP"))
         act(v("FS", 16, 256), v("FC", 16, 256), AF.Copy)
         if t == 0:
             fill(v("FS", 0, 16), 0.0)
@@ -434,7 +437,7 @@ def rank_program(g, core, T, topo):
         for y in range(16):
             mm(v("Y1", 256, 272), m128("EN", y), ("FS", y, 256, 16), False, y == 15)
         tt(v("O1"), v("TQ0"), v("NDUM"), A.max)
-        ts(v("NHK"), v("HK"), -1.0, A.mult)
+        ts(v("NHK"), v("HP"), -1.0, A.mult)
         tt(v("VS"), ind(v("X", 0, 4096), v("HKU")), v("A2", 0, 256), A.add)
         act(v("VB"), v("VS"), AF.Copy, bias=191.75, scale=0.5)
         if not last:
@@ -447,29 +450,26 @@ def rank_program(g, core, T, topo):
         else:
             tt(v("O1"), v("O1"), v("NHK"), A.min)
             output_lists()
+        if t == 0:
+            key_matrices()
         tt(v("O2"), v("Y1", 256, 272), v("NDUM"), A.max)
         tt(v("O3"), v("O2"), v("O1"), A.min)
         ts(v("OU"), v("O3"), -1.0, A.mult)
         tt(ind(v("X"), v("OU")), v("VB"), v("CN"), A.add)
         if last:
             dma("S", "d6", lambda q: q.dma_start(T.yx[:, :], T.X[:, 0:4096]), [v("X", 0, 4096)], [])
-            spread("UP", nu2)
             names()
-            ts(v("W1"), nu2, 8.0, A.mult)
-            ts(v("LX", 0, 256), v(po), 2048.0, A.add)
-            cp(v("LX", 256, 272), v("HK"))
+            ts(v("W1"), nu2, 8.0, A.mult, -2048.0, A.add)
+            cp(v("LP"), v(po))
+            cp(v("LX", 256, 272), nsc)
             tt(v("LX", 272, 288), v("W1"), npp, A.add)
-            cp(v("T3"), ind(v("LX", 0, 256), v("LL3R")))
+            tt(v("SM"), ind(v("LP"), v("LREV")), v(po), A.subtract)
+            tt(v("TM"), ind(v("UN"), v("LB")), v("SM"), A.mult)
+            tt(v("LX", 0, 256), v("TM"), v("LP"), A.add)
             cp(v("T1"), ind(v("LX"), v("LL3")))
-            tp(v("T4"), v("T3"))
             tp(v("T2"), v("T1"))
-            ts(v("NR"), ind(v("T4"), v("LL4", 0, 16)), 0.5, A.mult)
-            cp(v("KX"), ind(v("T2"), v("LL4")))
+            ts(v("KX"), ind(v("T2"), v("LL4")), 2048.0, A.add)
             dma("A", "d7", lambda q: q.dma_start(T.ys[:, :], T.KX[:, 256:272]), [v("KX", 256, 272)], [])
             dma("S", "d8", lambda q: q.dma_start(T.yp[:, :], T.KX[:, 272:288]), [v("KX", 272, 288)], [])
-            ts(v("NH"), v("KX", 0, 256), 0.5, A.mult)
-            tt(v("NH"), v("NR"), v("NH"), A.subtract)
-            tt(v("UP", 256, 512), v("UP", 0, 256), v("NH"), A.mult)
-            tt(v("YO"), v("UP", 256, 512), v("KX", 0, 256), A.add)
-            dma("A", "d9", lambda q: q.dma_start(T.yn[:, :], T.YO[:, :]), [v("YO")], [])
+            dma("A", "d9", lambda q: q.dma_start(T.yn[:, :], T.KX[:, 0:256]), [v("KX", 0, 256)], [])
     finish()

@@ -6,10 +6,10 @@ HO = 6
 F32, BF16, F16, I32, U16 = "float32", "bfloat16", "float16", "int32", "uint16"
 SCRATCH = {}
 for _n, _w, _d in (
-        ("X", 4352, BF16), ("DF", 4096, BF16), ("AB", 4096, BF16), ("EQ", 4096, F16),
+        ("X", 4352, BF16), ("DF", 4096, BF16), ("AB", 4096, BF16), ("EQ", 4096, BF16),
         ("EN", 2048, BF16), ("EF", 2048, BF16), ("TR", 2048, BF16), ("DK", 2048, F16), ("IJ", 2048, BF16),
         ("IT", 128, BF16), ("IB", 128, BF16), ("NB", 128, BF16), ("B32", 128, BF16),
-        ("BO", 128, BF16), ("BOS", 128, BF16), ("HF", 128, BF16), ("BG", 128, BF16), ("LREV", 16, U16),
+        ("BO", 128, BF16), ("BOS", 128, BF16), ("HF", 128, BF16), ("BG", 128, BF16), ("I4", 128, BF16), ("IP", 128, BF16), ("QC", 256, BF16), ("LREV", 16, U16),
         ("IC", 256, I32), ("PI", 8, I32), ("PF", 16, F32), ("MG", 256, I32), ("C1", 64, I32),
         ("LL1", 34, U16), ("LL2", 18, U16), ("LB", 16, U16), ("LL3", 36, U16), ("LL4", 18, U16), ("HPC", 16, F16),
         ("CN", 256, BF16), ("C63", 64, BF16), ("MB", 64, BF16), ("NT", 272, I32), ("KAPI", 1, I32), ("KC", 8, F32),
@@ -17,7 +17,7 @@ for _n, _w, _d in (
         ("T1", 576, F32), ("T2", 576, F32), ("T3", 288, F32), ("A2", 512, BF16),
         ("PR", 256, F32), ("ZI", 256, I32), ("HI", 256, I32), ("HU", 256, U16), ("KN", 256, I32), ("UU", 256, I32),
         ("TM", 256, F32), ("TX", 256, F32), ("SM", 256, F32), ("HKU", 16, U16), ("OU", 16, U16), ("BC", 16, F16),
-        ("MI", 16, F16), ("MK", 256, F32), ("TS", 256, F16), ("FS", 256, BF16), ("VS", 256, F32), ("VB", 256, BF16),
+        ("MI", 16, F16), ("MK", 256, F32), ("TS", 256, F16), ("FS", 256, BF16), ("XG", 256, BF16), ("VB", 256, BF16), ("ET", 1024, BF16), ("MJ", 16, F32),
         ("MC", 8, F32), ("MCI", 8, I32), ("LX", 288, F32), ("KX", 288, F32), ("LP", 256, F32), ("SMF", 512, F32), ("SMI", 128, I32)):
     SCRATCH[_n] = ("sbuf", [128, _w], _d)
 SMALL = {}
@@ -30,12 +30,12 @@ PSUM = ("Y0", "Y1", "ZP", "QP", "UP", "TP", "BPS", "FC")
 for _n in PSUM:
     SCRATCH[_n] = ("psum", [128, 512], F32)
 for _t in range(HO):
-    SCRATCH["S%d" % _t] = ("sbuf", [128, 80], F16)
+    SCRATCH["S%d" % _t] = ("sbuf", [128, 48], F16)
     SCRATCH["P%d" % _t] = ("sbuf", [128, 256], F16)
 for _r in range(4):
     SCRATCH["AR%d" % _r] = ("sbuf", [128, 512], BF16)
 for _t in range(2):
-    SCRATCH["SO%d" % _t] = ("sbuf", [128, 80], F16)
+    SCRATCH["SO%d" % _t] = ("sbuf", [128, 48], F16)
     SCRATCH["PO%d" % _t] = ("sbuf", [128, 256], F16)
 SEMAPHORES = (["cV", "cA", "cT", "cG"] + ["d%d" % i for i in range(12)] + ["rS%d" % t for t in range(1, HO)] +
               ["rP%d" % t for t in range(1, HO)] + ["rA%d" % r for r in range(4)] + ["lS%d" % t for t in range(1, HO)] +
@@ -73,7 +73,7 @@ def make_tracker(g, T):
                     if same or not ps:
                         if not (w or is_w) or hi <= l2 or h2 <= lo:
                             continue
-                        if same and (not w or (ps and eng == "T")):
+                        if same and eng == "T":
                             continue
                     if need.get(sem, 0) < val:
                         need[sem] = val
@@ -168,7 +168,10 @@ def rank_program(g, core, T, topo):
     def fill(out, c):
         op("V", lambda q: q.memset(ap(out), c), [], [out])
 
-    def act(out, in_, func, bias=0.0, scale=1.0):
+    def act(out, in_, func, bias=0.0, scale=1.0, accum=None):
+        if accum is not None:
+            op("A", lambda q: q.activation(ap(out), ap(in_), func, accum_out=ap(accum)), [in_], [out, accum])
+            return
         op("A", lambda q: q.activation(ap(out), ap(in_), func, bias=sc_(bias), scale=sc_(scale)), [in_, bias, scale], [out])
 
     def mm(out, l, r, start=True, stop=True):
@@ -244,48 +247,54 @@ def rank_program(g, core, T, topo):
     act(v("AN"), v("AA"), AF.Copy, scale=-0.5)
     act(v("RH"), v("RR"), AF.Copy, scale=0.5)
     act(v("BO"), v("BOS"), AF.Copy, scale=-1.0 / 524288.0)
-    for j in range(1, 16):
-        act(m128("IJ", j), v("IB"), AF.Copy, scale=4096.0 * j)
+    act(v("I4"), v("IB"), AF.Copy, scale=4096.0)
+    act(v("IP"), v("IB"), AF.Copy, scale=-16384.0)
+    for j in range(16):
+        act(m128("IJ", j), v("IB"), AF.Copy, scale=8192.0 * (15 - 2 * j))
     for y in range(16):
         act(m128("EF", y), v("BOS"), AF.Copy, scale=v("PEN", y, y + 1))
-    cp(v("T1", 0, 544), ind(v("NT"), v("LL1")))
-    tp(v("T2", 0, 544), v("T1", 0, 544))
     kc = [v("KC", i, i + 1) for i in range(3)]
+    ts(v("S0", 16, 48), v("IC", 0, 32), 0.0, A.mult)
+    ts(v("QC"), v("MG"), 4.0, A.mult, 2.0, A.add)
+    cp(v("T1", 0, 544), ind(v("NT"), v("LL1")))
     cp(kc[0], v("KAPI"))
+    tp(v("T2", 0, 544), v("T1", 0, 544))
     ts(kc[1], kc[0], 2048.0, A.is_ge, -4096.0, A.mult)
+    ts(v("S0", 0, 16), ind(v("T2", 0, 544), v("LL2", 16, 17)), -2048.0, A.add)
     tt(kc[2], kc[0], kc[1], A.add)
+    ts(v("P0"), ind(v("T2", 0, 544), v("LL2", 0, 16)), -2048.0, A.add)
     ts(v("PX"), v("MG"), p16, A.is_equal, kc[2], A.mult)
-    ts(v("T3", 0, 272), ind(v("T2", 0, 544), v("LL2", 0, 17)), -2048.0, A.add)
-    cp(v("S0", 0, 16), v("T3", 256, 272))
-    cp(v("P0"), v("T3", 0, 256))
-    for lo, c in ((16, 0.0), (32, 4.0), (48, 2.0), (64, 0.0)):
-        ts(v("S0", lo, lo + 16), v("IC", 0, 16), 0.0, A.mult, c, A.add)
     tt(v(me, 256, 512), v("RH"), v("AN"), A.add)
     for d in range(1, N):
         remote(T.cores[(rank + d) % N], me, me, "rA%d" % rank, "lA%d" % ((rank + d) % N))
 
-    def late_constants():
-        fill(v("MB"), 63.5)
-        fill(v("HF"), 0.5)
-        ts(r16, p16, -1.0, A.mult, 15.0, A.add)
-        ts(v("KR", 0, 16), v("PE16"), kc[2], A.mult)
-        ts(v("PR16"), v("IC", 0, 16), r16, A.is_equal)
-        ts(v("KR", 16, 32), v("PR16"), kc[2], A.mult)
-        mm(v("UP", 0, 32), v("BO"), v("KR"))
-        ts(v("LT16"), v("IC", 0, 16), p16, A.is_gt)
-        fill(v("CN"), -192.0)
-        ts(v("NDUM"), v("IC", 0, 16), -16.0, A.mult, p16, A.subtract)
-        fill(v("C63"), 63.5)
-        ts(v("NDUM"), v("NDUM"), -4096.0, A.add)
+    kl2 = (SMALL["KL"][0], SMALL["KL"][1], SMALL["KL"][1] + 32, 1)
+    small = [
+        lambda: ts(r16, p16, -1.0, A.mult, 15.0, A.add),
+        lambda: ts(v("KR", 0, 16), v("PE16"), kc[2], A.mult),
+        lambda: ts(v("PR16"), v("IC", 0, 16), r16, A.is_equal),
+        lambda: fill(v("MB"), 63.5),
+        lambda: (ts(v("KR", 16, 32), v("PR16"), kc[2], A.mult), mm(v("UP", 0, 32), v("BO"), v("KR"))),
+        lambda: fill(v("HF"), 0.5),
+        lambda: ts(v("NDUM"), v("IC", 0, 16), -16.0, A.mult, p16, A.subtract),
+        lambda: cp(kl2, v("UP", 0, 32)),
+        lambda: ts(v("LT16"), v("IC", 0, 16), p16, A.is_gt),
+        lambda: tt(v("KD"), v("KLR"), v("KL"), A.subtract),
+        lambda: ts(v("NDUM"), v("NDUM"), -4096.0, A.add),
+        lambda: ts(v("KE"), v("KD"), 2048.0, A.is_ge, -4096.0, A.mult),
+        lambda: fill(v("C63"), 63.5),
+        lambda: tt(v("KE"), v("KE"), v("KD"), A.add),
+        lambda: fill(v("CN"), -192.0),
+        lambda: ts(v("KD"), v("KE"), -2048.0, A.is_lt, 4096.0, A.mult),
+        lambda: tt(v("KD"), v("KE"), v("KD"), A.add),
+        lambda: ts(v("KD"), v("KD"), 16.0, A.mult)]
+
+    def filler(n):
+        for _ in range(n):
+            if small:
+                small.pop(0)()
 
     def key_matrices():
-        cp((SMALL["KL"][0], SMALL["KL"][1], SMALL["KL"][1] + 32, 1), v("UP", 0, 32))
-        tt(v("KD"), v("KLR"), v("KL"), A.subtract)
-        ts(v("KE"), v("KD"), 2048.0, A.is_ge, -4096.0, A.mult)
-        tt(v("KE"), v("KE"), v("KD"), A.add)
-        ts(v("KD"), v("KE"), -2048.0, A.is_lt, 4096.0, A.mult)
-        tt(v("KD"), v("KE"), v("KD"), A.add)
-        ts(v("KD"), v("KD"), 16.0, A.mult)
         for j in range(16):
             ts(m128("DK", j), v("IB"), v("KD", j, j + 1), A.mult)
 
@@ -303,10 +312,12 @@ def rank_program(g, core, T, topo):
         for y in range(16):
             mm((out, y, 256, 16), m128("EF", y), src)
 
+    on_scalar = [1, 2, 3]
+    order = [b for b in range(16) if b not in on_scalar] + on_scalar
     for t in range(HO):
         last = t == HO - 1
         S, P = "S%d" % t, "P%d" % t
-        sc, u2, e4, w4, pp = [v(S, 16 * i, 16 * i + 16) for i in range(5)]
+        sc, u2, pp = [v(S, 16 * i, 16 * i + 16) for i in range(3)]
         ar = "AR%d" % ((rank - t) % N)
         so, po = "SO%d" % (t % 2), "PO%d" % (t % 2)
         mm(v("ZP", 0, 256), v("B32"), v("PX"), True, False)
@@ -317,25 +328,31 @@ def rank_program(g, core, T, topo):
         if t:
             spread("UP", u2)
         ts(v("S32"), sc, 2080.0, A.add)
-        ts(v("SF"), sc, 2048.0, A.add)
+        filler(1)
         tt(v("PR"), ind(v("S32"), v("LB")), v(P), A.mult)
-        ts(v("WB"), v("SF"), 32.0, A.mult, float((25952 * t) % 131072 - 262144), A.add)
-        tt(v("ZI"), v("PR"), v("ZP", 0, 256), A.add)
         if t == 0:
             cp(v("A2", 0, 256), v(ar, 0, 256))
-        ts(v("HI"), v("ZI"), 5, A.arith_shift_right, 4095, A.bitwise_and)
+            filler(2)
+        halves = ((0, 128), (128, 256))
+        for h in halves:
+            tt(v("ZI", *h), v("PR", *h), v("ZP", *h), A.add)
         if t:
             tt(v("UP", 256, 512), v("UP", 0, 256), v(ar, 256, 512), A.mult)
-        cp(v("HU"), v("HI"))
+        filler(2)
+        for h in halves:
+            ts(v("HI", *h), v("ZI", *h), 5, A.arith_shift_right, 4095, A.bitwise_and)
         if t:
             tt(v("A2", 0, 256), v("UP", 256, 512), v(ar, 0, 256), A.add)
-        cp(v("A2", 256, 512), v("A2", 0, 256))
-        if t == 0:
-            late_constants()
+        act(v("A2", 256, 512), v("A2", 0, 256), AF.Copy)
+        filler(2)
+        for h in halves:
+            cp(v("HU", *h), v("HI", *h))
+        filler(2)
+        mm(v("QP", 0, 256), v("I4"), v("QC"), True, False)
         for j in range(16):
-            if j:
-                mm(blk("QP", j), m128("IJ", j), e4, True, False)
-            mm(blk("QP", j), m128("IJ", 1), w4, j == 0, True)
+            if t:
+                mm(blk("QP", j), m128("IJ", j), u2, False, False)
+            mm(blk("QP", j), v("IP"), pp, False, j == 15)
         act(v("DF", 0, 768), ind(v("X", 0, 4096), v("HU", 0, 48)), AF.Copy)
         mm(v("FC"), v("IB"), v("DF", 0, 512), True, False)
         mm(v("FC"), v("NB"), v("A2"), False, True)
@@ -358,9 +375,15 @@ def rank_program(g, core, T, topo):
         if t == 0:
             for y in range(16):
                 act(m128("TR", y), m128("EN", y), AF.Copy, scale=v("LT16", y, y + 1))
-        tt(v("KN"), v("QP", 0, 256), v("HI"), A.add)
-        ts(v("UU"), v("KN"), 0xFFFFFF, A.bitwise_and)
+        for h in halves:
+            tt(v("KN", *h), v("QP", *h), v("HI", *h), A.add)
+        filler(1)
+        for h in halves:
+            ts(v("UU", *h), v("KN", *h), 0xFFFFFF, A.bitwise_and)
+        filler(1)
         tt(v("TM", 0, 128), v("UU", 0, 128), v("UU", 128, 256), A.min)
+        ts(v("SF"), sc, 2048.0, A.add)
+        filler(1)
         tt(v("TM", 128, 192), v("TM", 0, 64), v("TM", 64, 128), A.min)
         tt(v("SM", 0, 192), v("KN", 0, 192), v("Y0", 0, 192), A.min)
         tt(v("TM", 192, 224), v("TM", 128, 160), v("TM", 160, 192), A.min)
@@ -372,63 +395,78 @@ def rank_program(g, core, T, topo):
         tt(v("TX", 144, 160), v("TX", 96, 112), v("TX", 112, 128), A.max)
         ts(v("HP"), v("TM", 224, 240), -8192.0, A.add)
         tt(v("TX", 160, 176), v("TX", 128, 144), v("TX", 144, 160), A.max)
+        cp(v("HKU"), v("HP"))
+        act(v("XG"), ind(v("X", 0, 4096), v("HKU")), AF.Copy)
+        mm(v("QP", 256, 512), v("IB"), v("XG"), True, False)
+        mm(v("QP", 256, 512), v("IB"), v("A2", 0, 256), False, True)
+        act(v("NHK"), v("HP"), AF.Copy, scale=-1.0)
         tt(v("SM", 192, 256), v("KN", 192, 256), v("Y1", 0, 64), A.min)
         tt(v("TX", 176, 192), v("TX", 160, 176), v("HP"), A.max)
         tt(v("TX", 192, 224), v("SM", 192, 224), v("SM", 224, 256), A.max)
+        ts(v("WB"), v("SF"), 32.0, A.mult, float((25952 * t) % 131072 - 262144), A.add)
         tt(v("TX", 224, 240), v("TX", 192, 208), v("TX", 176, 192), A.max)
+        filler(1)
         tt(v("MM"), v("TX", 208, 224), v("TX", 224, 240), A.max)
-        nsc, nu2, ne4, nw4, npp = [v(so, 16 * i, 16 * i + 16) for i in range(5)]
+        filler(99)
+        nsc, nu2, npp = [v(so, 16 * i, 16 * i + 16) for i in range(3)]
         ts(v("HK"), v("MM"), 4095, A.bitwise_and)
         ts(v("DL"), v("MM"), 14, A.arith_shift_right)
-        ts(v("MI"), v("MM"), 8192.0, A.is_lt, 2.0, A.mult)
         tt(v("BP"), v("SF"), v("HK"), A.mult)
-        ts(nsc, v("HK"), -2048.0, A.add)
         tt(v("KS"), pp, v("DL"), A.add)
         tt(v("BZ"), v("BP"), v("WB"), A.add)
-        ts(v("LIM"), v("DL"), 16384.0, A.mult, 16383.0, A.add)
-        ts(v("KQ"), v("KS"), 15.0, A.is_equal, 2.0, A.mult)
+        ts(v("MI"), v("MM"), 8192.0, A.is_lt, 2.0, A.mult)
+        act(v("W1"), v("KS"), AF.Copy, scale=-1.0, bias=7.0)
+        act(v("W3"), v("KS"), AF.Copy, bias=1.0)
         ts(v("BI"), v("BZ"), 5, A.arith_shift_right, 4095, A.bitwise_and)
-        ts(v("W1"), v("KS"), -1.0, A.mult, 7.0, A.add)
-        tt(v("TU"), v("KQ"), v("MI"), A.max)
+        ts(v("KQ"), v("KS"), 15.0, A.is_equal, 2.0, A.mult)
         ts(v("BC"), v("BI"), -2048.0, A.add)
         for j in range(16):
             mm(blk("BPS", j), v("IB"), v("BC"), False, j == 15)
-        ts(v("W3"), v("KS"), 1.0, A.add)
+        if not last:
+            mm(v("Y0", 256, 272), v("HF"), v("MI"))
+        tt(v("TU"), v("KQ"), v("MI"), A.max)
+        ts(v("TQ0"), v("MM"), 8192.0, A.is_ge, -12000.0, A.mult)
         tt(v("UN"), u2, v("TU"), A.not_equal)
         tt(v("W2"), v("W1"), v("TU"), A.mult)
-        ts(v("TQ0"), v("MM"), 8192.0, A.is_ge, -12000.0, A.mult)
         ts(nu2, v("UN"), 2.0, A.mult)
         tt(npp, v("W2"), v("W3"), A.add)
+        ts(nsc, v("HK"), -2048.0, A.add)
         if not last:
-            ts(v("W4"), v("UN"), 15.0, A.mult)
-            ts(ne4, v("UN"), -8.0, A.mult, 4.0, A.add)
-            tt(v("W5"), v("W4"), npp, A.subtract)
-            tt(v("TQ"), v("TQ0"), v("HPC"), A.add)
-            ts(nw4, v("W5"), 4.0, A.mult, 2.0, A.add)
             remote(nxt, "S%d" % (t + 1), so, "rS%d" % (t + 1), "lS%d" % (t + 1))
-            mm(v("Y0", 256, 272), v("HF"), v("MI"))
-        else:
-            tt(v("TQ"), v("TQ0"), v("HPC"), A.add)
+        tt(v("TQ"), v("TQ0"), v("HPC"), A.add)
+        cp(v("TS"), v("TP", 0, 256))
+        for b in on_scalar:
+            act(v("ET", 272 * b, 256 * b + 256), v("TP", 16 * b, 256), AF.Abs, scale=-1.0, bias=v("TQ", b, b + 1))
+        for b in on_scalar:
+            act(v("EQ", 272 * b, 256 * b + 256), v("ET", 272 * b, 256 * b + 256), AF.Relu, scale=-1.0, bias=1.0)
+        if not last:
+            act(v("MJ"), v("Y0", 256, 272), AF.Copy, accum=v("MC", 0, 1))
+        ts(v("LIM"), v("DL"), 16384.0, A.mult, 16383.0, A.add)
 
         def names():
             tt(v("MK"), ind(v("LIM"), v("LB")), v("UU"), A.is_ge)
-            tt(v("BPS", 256, 512), v("BPS", 0, 256), v("MK"), A.mult)
-            tt(v(po), v("BPS", 256, 512), v(P), A.add)
+            for lo in (0, 128):
+                tt(v("BPS", 256 + lo, 384 + lo), v("BPS", lo, lo + 128), v("MK", lo, lo + 128), A.mult)
+            for lo in (0, 128):
+                tt(v(po, lo, lo + 128), v("BPS", 256 + lo, 384 + lo), v(P, lo, lo + 128), A.add)
 
         def compare(bs):
             for b in bs:
-                ts(v("EQ", 272 * b, 256 * b + 256), v("TS", 16 * b, 256), v("TQ", b, b + 1), A.is_equal)
+                if b not in on_scalar:
+                    ts(v("EQ", 272 * b, 256 * b + 256), v("TS", 16 * b, 256), v("TQ", b, b + 1), A.is_equal)
                 if b < 15:
-                    mm(v("FC", 16 * b + 16, 256), v("BO"), v("EQ", 272 * b + 16, 256 * b + 256), b == 0, b == 14)
+                    mm(v("FC", 16 * b + 16, 256), v("BO"), v("EQ", 272 * b + 16, 256 * b + 256), b == 0, b == order[-1])
 
-        cp(v("TS"), v("TP", 0, 256))
         if last:
-            compare(range(16))
+            compare(order)
+            names()
+            cp(v("LP"), v(po))
         else:
+            compare(order[:1])
             names()
             remote(nxt, "P%d" % (t + 1), po, "rP%d" % (t + 1), "lP%d" % (t + 1))
-            compare(range(16))
-        cp(v("HKU"), v("HP"))
+            compare(order[1:])
+        act(v("VB"), v("QP", 256, 512), AF.Copy, bias=191.75, scale=0.5)
         act(v("FS", 16, 256), v("FC", 16, 256), AF.Copy)
         if t == 0:
             fill(v("FS", 0, 16), 0.0)
@@ -437,11 +475,7 @@ def rank_program(g, core, T, topo):
         for y in range(16):
             mm(v("Y1", 256, 272), m128("EN", y), ("FS", y, 256, 16), False, y == 15)
         tt(v("O1"), v("TQ0"), v("NDUM"), A.max)
-        ts(v("NHK"), v("HP"), -1.0, A.mult)
-        tt(v("VS"), ind(v("X", 0, 4096), v("HKU")), v("A2", 0, 256), A.add)
-        act(v("VB"), v("VS"), AF.Copy, bias=191.75, scale=0.5)
         if not last:
-            op("V", lambda q: q.tensor_reduce(T.MC[:, 0:1], T.Y0[:, 256:272], AxisListType.X, A.add), [v("Y0", 256, 272)], [v("MC", 0, 1)])
             tt(v("O1"), v("O1"), v("NHK"), A.min)
             cp(v("MCI", 0, 1), v("MC", 0, 1))
             ts(v("MCI", 1, 2), v("MCI", 0, 1), 15, A.bitwise_and)
@@ -449,6 +483,7 @@ def rank_program(g, core, T, topo):
             act(v("MB"), v("C63"), AF.Identity, bias=v("MC", 1, 2))
         else:
             tt(v("O1"), v("O1"), v("NHK"), A.min)
+        if t == 1:
             output_lists()
         if t == 0:
             key_matrices()
@@ -458,9 +493,7 @@ def rank_program(g, core, T, topo):
         tt(ind(v("X"), v("OU")), v("VB"), v("CN"), A.add)
         if last:
             dma("S", "d6", lambda q: q.dma_start(T.yx[:, :], T.X[:, 0:4096]), [v("X", 0, 4096)], [])
-            names()
             ts(v("W1"), nu2, 8.0, A.mult, -2048.0, A.add)
-            cp(v("LP"), v(po))
             cp(v("LX", 256, 272), nsc)
             tt(v("LX", 272, 288), v("W1"), npp, A.add)
             tt(v("SM"), ind(v("LP"), v("LREV")), v(po), A.subtract)

import numpy as np
from concourse.bass import DstId, RemoteDMATransfer
from concourse.mybir import dt, AluOpType, AxisListType, ActivationFunctionType

HO = 6
F32, BF16, F16, I32, U16 = "float32", "bfloat16", "float16", "int32", "uint16"
SCRATCH = {}
for _n, _w, _d in (
        ("X", 4352, BF16), ("DF", 4096, BF16), ("AB", 4096, BF16), ("EQ", 4096, BF16),
        ("EN", 2048, BF16), ("EF", 2048, BF16), ("TR", 2048, BF16), ("DK", 2048, F16), ("IJ", 2048, BF16),
        ("IT", 128, BF16), ("IB", 128, BF16), ("NB", 128, BF16), ("B32", 128, BF16),
        ("BO", 128, BF16), ("BOS", 128, BF16), ("HF", 128, BF16), ("BG", 128, BF16), ("I4", 128, BF16), ("IP", 128, BF16), ("QC", 256, BF16), ("LREV", 16, U16),
        ("IC", 256, I32), ("PI", 8, I32), ("PF", 16, F32), ("MG", 256, I32), ("C1", 64, I32),
        ("LL1", 34, U16), ("LL2", 18, U16), ("LB", 16, U16), ("LL3", 36, U16), ("LL4", 18, U16), ("HPC", 16, F16),
        ("CN", 256, BF16), ("C63", 64, BF16), ("MB", 64, BF16), ("NT", 272, I32), ("KAPI", 1, I32), ("KC", 8, F32),
        ("KR", 32, F16), ("PX", 256, F16), ("AA", 256, BF16), ("RR", 256, BF16), ("RH", 256, BF16), ("AN", 256, BF16),
        ("T1", 576, F32), ("T2", 576, F32), ("T3", 288, F32), ("A2", 512, BF16),
        ("PR", 256, F32), ("ZI", 256, I32), ("HI", 256, I32), ("HU", 256, U16), ("KN", 256, I32), ("UU", 256, I32),
        ("TM", 256, F32), ("TX", 256, F32), ("SM", 256, F32), ("HKU", 16, U16), ("OU", 16, U16), ("BC", 16, F16),
        ("MI", 16, F16), ("MK", 256, F32), ("TS", 256, F16), ("FS", 256, BF16), ("XG", 256, BF16), ("VB", 256, BF16), ("ET", 1024, BF16), ("MJ", 16, F32),
        ("MC", 8, F32), ("MCI", 8, I32), ("LX", 288, F32), ("KX", 288, F32), ("LP", 256, F32), ("SMF", 512, F32), ("SMI", 128, I32)):
    SCRATCH[_n] = ("sbuf", [128, _w], _d)
SMALL = {}
for _i, _n in enumerate(("PE16", "PEN", "PR16", "LT16", "KL", "KLR", "KD", "KE", "NDUM", "S32", "SF", "WB", "HP", "BP", "LIM", "KS", "KQ", "TU",
                         "UN", "W1", "W2", "W3", "W4", "W5", "TQ", "TQ0", "O1", "O2", "O3", "NHK")):
    SMALL[_n] = ("SMF", 16 * _i)
for _i, _n in enumerate(("MM", "HK", "BZ", "BI", "DL")):
    SMALL[_n] = ("SMI", 16 * _i)
PSUM = ("Y0", "Y1", "ZP", "QP", "UP", "TP", "BPS", "FC")
for _n in PSUM:
    SCRATCH[_n] = ("psum", [128, 512], F32)
for _t in range(HO):
    SCRATCH["S%d" % _t] = ("sbuf", [128, 48], F16)
    SCRATCH["P%d" % _t] = ("sbuf", [128, 256], F16)
for _r in range(4):
    SCRATCH["AR%d" % _r] = ("sbuf", [128, 512], BF16)
for _t in range(2):
    SCRATCH["SO%d" % _t] = ("sbuf", [128, 48], F16)
    SCRATCH["PO%d" % _t] = ("sbuf", [128, 256], F16)
SEMAPHORES = (["cV", "cA", "cT", "cG"] + ["d%d" % i for i in range(12)] + ["rS%d" % t for t in range(1, HO)] +
              ["rP%d" % t for t in range(1, HO)] + ["rA%d" % r for r in range(4)] + ["lS%d" % t for t in range(1, HO)] +
              ["lP%d" % t for t in range(1, HO)] + ["lA%d" % r for r in range(4)])


def make_tracker(g, T):
    queue = {"V": g.vector, "A": g.scalar, "T": g.tensor, "G": g, "S": g.sync}
    count = {"V": 0, "A": 0, "T": 0, "G": 0}
    know = {e: {} for e in queue}
    snap = {}
    hist = {}
    allsem = {}

    def ap(v):
        if v[0] == "ind":
            return ap(v[1]).indirect(ap(v[2]))
        t = T[v[0]]
        return t[:, v[1]:v[2]] if v[3] == 1 else t[:, v[1]:v[2]:v[3]]

    def flat(vs):
        out = []
        for v in vs:
            if isinstance(v, tuple):
                out += [v[1], v[2]] if v[0] == "ind" else [v]
        return out

    def deps(eng, reads, writes):
        need = {}
        for is_w, vs in ((False, reads), (True, writes)):
            for (b, lo, hi, st) in vs:
                ps = b in PSUM
                for (w, e, l2, h2, sem, val) in hist.get(b, ()):
                    same = e == eng and eng in count
                    if same or not ps:
                        if not (w or is_w) or hi <= l2 or h2 <= lo:
                            continue
                        if same and eng == "T":
                            continue
                    if need.get(sem, 0) < val:
                        need[sem] = val
        return need

    def wait(eng, need):
        kn = know[eng]
        for sem in sorted(need, key=lambda s: (-len(snap.get((s, need[s]), ())), s)):
            val = need[sem]
            if kn.get(sem, 0) >= val:
                continue
            queue[eng].wait_ge(T.sem[sem], val)
            kn[sem] = val
            for s2, v2 in snap.get((sem, val), {}).items():
                if kn.get(s2, 0) < v2:
                    kn[s2] = v2

    def note(eng, reads, writes, sem, val, kn):
        for is_w, vs in ((True, writes), (False, reads)):
            for (b, lo, hi, st) in vs:
                h = hist.setdefault(b, [])
                if eng != "dma":
                    if is_w and st == 1 and b not in PSUM:
                        h[:] = [x for x in h if not (lo <= x[2] and x[3] <= hi)]
                    h[:] = [x for x in h if not (x[1] == eng and x[0] == is_w and x[2] == lo and x[3] == hi)]
                h.append((is_w, eng, lo, hi, sem, val))
        snap[(sem, val)] = dict(kn)
        allsem[sem] = val

    def op(eng, fn, reads, writes):
        reads, writes = flat(reads), flat(writes)
        wait(eng, deps(eng, reads, writes))
        count[eng] += 1
        fn(queue[eng]).then_inc(T.sem["c" + eng], 1)
        note(eng, reads, writes, "c" + eng, count[eng], know[eng])

    def dma(eng, sem, fn, reads, writes):
        wait(eng, deps("dma", reads, writes))
        fn(queue[eng]).then_inc(T.sem[sem], 16)
        note("dma", reads, writes, sem, 16, know[eng])

    def send(fn, reads, sem, val):
        wait("G", deps("dma", reads, []))
        fn(g)
        note("dma", reads, [], sem, val, know["G"])

    def arrival(v, sem, val):
        note("dma", [], [v], sem, val, {})

    def finish():
        for sem in sorted(allsem):
            wait("G", {sem: allsem[sem]})
    return ap, op, dma, send, arrival, finish


def rank_program(g, core, T, topo):
    rank = T.rank_of(core)
    if rank is None:
        return
    N = len(T.cores)
    A = AluOpType
    AF = ActivationFunctionType
    ap, op, dma, send, arrival, finish = make_tracker(g, T)

    def v(b, lo=0, hi=None, st=1):
        if b in SMALL:
            n, base = SMALL[b]
            return (n, base + lo, base + (16 if hi is None else hi), st)
        return (b, lo, SCRATCH[b][1][1] if hi is None else hi, st)

    def ind(w, o):
        return ("ind", w, o)

    def sc_(x):
        return ap(x) if isinstance(x, tuple) else x

    def ts(out, in0, s1, op0, s2=None, op1=None):
        if op1 is None:
            op("V", lambda q: q.tensor_scalar(ap(out), ap(in0), sc_(s1), None, op0), [in0, s1], [out])
        else:
            op("V", lambda q: q.tensor_scalar(ap(out), ap(in0), sc_(s1), sc_(s2), op0, op1), [in0, s1, s2], [out])

    def tt(out, in0, in1, o):
        if out[0] == "ind":
            op("V", lambda q: q.tensor_tensor(ap(out), ap(in0), ap(in1), o), [in0, in1, out[2]], [out[1]])
        else:
            op("V", lambda q: q.tensor_tensor(ap(out), ap(in0), ap(in1), o), [in0, in1], [out])

    def cp(out, in_):
        op("V", lambda q: q.tensor_copy(ap(out), ap(in_)), [in_], [out])

    def fill(out, c):
        op("V", lambda q: q.memset(ap(out), c), [], [out])

    def act(out, in_, func, bias=0.0, scale=1.0, accum=None):
        if accum is not None:
            op("A", lambda q: q.activation(ap(out), ap(in_), func, accum_out=ap(accum)), [in_], [out, accum])
            return
        op("A", lambda q: q.activation(ap(out), ap(in_), func, bias=sc_(bias), scale=sc_(scale)), [in_, bias, scale], [out])

    def mm(out, l, r, start=True, stop=True):
        op("T", lambda q: q.matmul(ap(out), ap(l), ap(r), start, stop), [l, r], [out])

    def tp(out, in_):
        op("V", lambda q: q.transpose(ap(out), ap(in_)), [in_], [out])

    def iota(out, pattern, cm):
        op("G", lambda q: q.iota(ap(out), pattern, 0, cm), [], [out])

    def m128(b, j):
        return v(b, 128 * j, 128 * j + 128)

    def blk(b, j):
        return v(b, 16 * j, 16 * j + 16)

    def remote(dst, ob, ib, rsem, lsem):
        rid, pid, _ = topo.addr(dst)
        msk = topo.mask(core, dst)
        send(lambda q: q.remote_dma(out_ap=T[ob][:], in_ap=T[ib][:], remote_sem=T.sem[rsem], local_sem=T.sem[lsem],
                                    pid=pid, routing_id=rid, dma_engine_mask=msk), [v(ib)], lsem, len(topo.engines(core, dst)))

    def incs(src, dst):
        return len(topo.engines(src, dst))

    nxt, prv = T.cores[(rank + 1) % N], T.cores[(rank - 1) % N]
    for t in range(1, HO):
        arrival(v("S%d" % t), "rS%d" % t, incs(prv, core))
        arrival(v("P%d" % t), "rP%d" % t, incs(prv, core))
    for r in range(N):
        if r != rank:
            arrival(v("AR%d" % r), "rA%d" % r, incs(T.cores[r], core))

    dma("A", "d0", lambda q: q.dma_start(T.NT[:, 0:256], T.pn[:, :]), [], [v("NT", 0, 256)])
    dma("S", "d1", lambda q: q.dma_start(T.NT[:, 256:272], T.s0[:, :]), [], [v("NT", 256, 272)])
    dma("A", "d2", lambda q: q.dma_start(T.KAPI[:, :], T.kap[:, :]), [], [v("KAPI")])
    dma("S", "d5", lambda q: q.dma_start(T.X[:, 0:4096], T.x[:, :]), [], [v("X", 0, 4096)])
    dma("A", "d3", lambda q: q.dma_start(T.AA[:, :], T.a0[:, :]), [], [v("AA")])
    dma("A", "d4", lambda q: q.dma_start(T.RR[:, :], T.r0[:, :]), [], [v("RR")])
    me = "AR%d" % rank

    iota(v("IC"), [[1, 256]], 0)
    iota(v("PI", 0, 1), [[1, 1]], 1)
    pI = v("PI", 0, 1)
    ts(v("PI", 1, 2), pI, 15, A.bitwise_and)
    ts(v("PI", 2, 3), pI, 4, A.arith_shift_right)
    ts(v("PI", 3, 4), pI, 4, A.arith_shift_right, 1, A.bitwise_and)
    ts(v("C1"), v("IC", 0, 64), 1, A.arith_shift_right)
    cp(v("PF", 0, 4), v("PI", 0, 4))
    pf, p16, pg, hf = [v("PF", i, i + 1) for i in range(4)]
    h16, x32, y32, k16, r16 = [v("PF", i, i + 1) for i in range(4, 9)]
    ts(v("LL1"), v("C1", 0, 34), 16.0, A.mult, p16, A.add)
    ts(v("MG"), v("IC"), 4, A.arith_shift_right)
    ts(h16, hf, 16.0, A.mult, p16, A.add)
    ts(v("IB"), v("IC", 0, 128), pf, A.is_equal)
    ts(v("BOS"), v("MG", 0, 128), pg, A.is_equal, -524288.0, A.mult)
    ts(v("PE16"), v("IC", 0, 16), p16, A.is_equal)
    ts(x32, p16, 31.0, A.mult, h16, A.add)
    ts(y32, h16, 512.0, A.add)
    ts(v("PEN"), v("PE16"), -1.0 / 524288.0, A.mult)
    ts(v("LL2", 0, 16), v("IC", 0, 16), x32, A.add)
    ts(v("LL2", 16, 17), v("IC", 0, 1), y32, A.add)
    ts(v("LB"), v("IC", 0, 16), 0.0, A.mult, p16, A.add)
    for y in range(16):
        op("G", lambda q, y=y: q.affine_select(ap(m128("EN", y)), ap(v("BOS")), [[0, 8], [1, 16]], A.is_equal, 0.0, -y, 0),
           [v("BOS")], [m128("EN", y)])
    act(v("B32"), v("BOS"), AF.Copy, scale=-32.0 / 524288.0)
    act(v("IT"), v("IB"), AF.Copy, scale=3232.0)
    act(v("NB"), v("IB"), AF.Copy, scale=-1.0)
    act(v("BG"), v("IB"), AF.Copy, scale=524288.0)
    act(v(me, 0, 256), v("AA"), AF.Copy)
    act(v("AN"), v("AA"), AF.Copy, scale=-0.5)
    act(v("RH"), v("RR"), AF.Copy, scale=0.5)
    act(v("BO"), v("BOS"), AF.Copy, scale=-1.0 / 524288.0)
    act(v("I4"), v("IB"), AF.Copy, scale=4096.0)
    act(v("IP"), v("IB"), AF.Copy, scale=-16384.0)
    for j in range(16):
        act(m128("IJ", j), v("IB"), AF.Copy, scale=8192.0 * (15 - 2 * j))
    for y in range(16):
        act(m128("EF", y), v("BOS"), AF.Copy, scale=v("PEN", y, y + 1))
    kc = [v("KC", i, i + 1) for i in range(3)]
    ts(v("S0", 16, 48), v("IC", 0, 32), 0.0, A.mult)
    ts(v("QC"), v("MG"), 4.0, A.mult, 2.0, A.add)
    cp(v("T1", 0, 544), ind(v("NT"), v("LL1")))
    cp(kc[0], v("KAPI"))
    tp(v("T2", 0, 544), v("T1", 0, 544))
    ts(kc[1], kc[0], 2048.0, A.is_ge, -4096.0, A.mult)
    ts(v("S0", 0, 16), ind(v("T2", 0, 544), v("LL2", 16, 17)), -2048.0, A.add)
    tt(kc[2], kc[0], kc[1], A.add)
    ts(v("P0"), ind(v("T2", 0, 544), v("LL2", 0, 16)), -2048.0, A.add)
    ts(v("PX"), v("MG"), p16, A.is_equal, kc[2], A.mult)
    tt(v(me, 256, 512), v("RH"), v("AN"), A.add)
    for d in range(1, N):
        remote(T.cores[(rank + d) % N], me, me, "rA%d" % rank, "lA%d" % ((rank + d) % N))

    kl2 = (SMALL["KL"][0], SMALL["KL"][1], SMALL["KL"][1] + 32, 1)
    small = [
        lambda: ts(r16, p16, -1.0, A.mult, 15.0, A.add),
        lambda: ts(v("KR", 0, 16), v("PE16"), kc[2], A.mult),
        lambda: ts(v("PR16"), v("IC", 0, 16), r16, A.is_equal),
        lambda: fill(v("MB"), 63.5),
        lambda: (ts(v("KR", 16, 32), v("PR16"), kc[2], A.mult), mm(v("UP", 0, 32), v("BO"), v("KR"))),
        lambda: fill(v("HF"), 0.5),
        lambda: ts(v("NDUM"), v("IC", 0, 16), -16.0, A.mult, p16, A.subtract),
        lambda: cp(kl2, v("UP", 0, 32)),
        lambda: ts(v("LT16"), v("IC", 0, 16), p16, A.is_gt),
        lambda: tt(v("KD"), v("KLR"), v("KL"), A.subtract),
        lambda: ts(v("NDUM"), v("NDUM"), -4096.0, A.add),
        lambda: ts(v("KE"), v("KD"), 2048.0, A.is_ge, -4096.0, A.mult),
        lambda: fill(v("C63"), 63.5),
        lambda: tt(v("KE"), v("KE"), v("KD"), A.add),
        lambda: fill(v("CN"), -192.0),
        lambda: ts(v("KD"), v("KE"), -2048.0, A.is_lt, 4096.0, A.mult),
        lambda: tt(v("KD"), v("KE"), v("KD"), A.add),
        lambda: ts(v("KD"), v("KD"), 16.0, A.mult)]

    def filler(n):
        for _ in range(n):
            if small:
                small.pop(0)()

    def key_matrices():
        for j in range(16):
            ts(m128("DK", j), v("IB"), v("KD", j, j + 1), A.mult)

    def output_lists():
        ts(k16, p16, 16.0, A.mult)
        ts(r16, p16, 240.0, A.add)
        ts(v("LREV"), v("IC", 0, 16), -16.0, A.mult, r16, A.add)
        ts(v("LL3", 0, 32), v("C1", 0, 32), k16, A.add)
        ts(v("LL3", 32, 34), v("IC", 0, 2), 0.0, A.mult, p16, A.add)
        ts(v("LL3", 32, 34), v("LL3", 32, 34), 256.0, A.add)
        ts(v("LL3", 34, 36), v("LL3", 32, 34), 16.0, A.add)
        ts(v("LL4"), v("IC", 0, 18), 32.0, A.mult, h16, A.add)

    def spread(out, src):
        for y in range(16):
            mm((out, y, 256, 16), m128("EF", y), src)

    on_scalar = [1, 2, 3]
    order = [b for b in range(16) if b not in on_scalar] + on_scalar
    for t in range(HO):
        last = t == HO - 1
        S, P = "S%d" % t, "P%d" % t
        sc, u2, pp = [v(S, 16 * i, 16 * i + 16) for i in range(3)]
        ar = "AR%d" % ((rank - t) % N)
        so, po = "SO%d" % (t % 2), "PO%d" % (t % 2)
        mm(v("ZP", 0, 256), v("B32"), v("PX"), True, False)
        for j in range(16):
            mm(blk("ZP", j), v("IT"), sc, False, t == 0 and j == 15)
            if t:
                mm(blk("ZP", j), m128("DK", j), u2, False, j == 15)
        if t:
            spread("UP", u2)
        ts(v("S32"), sc, 2080.0, A.add)
        filler(1)
        tt(v("PR"), ind(v("S32"), v("LB")), v(P), A.mult)
        if t == 0:
            cp(v("A2", 0, 256), v(ar, 0, 256))
            filler(2)
        halves = ((0, 128), (128, 256))
        for h in halves:
            tt(v("ZI", *h), v("PR", *h), v("ZP", *h), A.add)
        if t:
            tt(v("UP", 256, 512), v("UP", 0, 256), v(ar, 256, 512), A.mult)
        filler(2)
        for h in halves:
            ts(v("HI", *h), v("ZI", *h), 5, A.arith_shift_right, 4095, A.bitwise_and)
        if t:
            tt(v("A2", 0, 256), v("UP", 256, 512), v(ar, 0, 256), A.add)
        act(v("A2", 256, 512), v("A2", 0, 256), AF.Copy)
        filler(2)
        for h in halves:
            cp(v("HU", *h), v("HI", *h))
        filler(2)
        mm(v("QP", 0, 256), v("I4"), v("QC"), True, False)
        for j in range(16):
            if t:
                mm(blk("QP", j), m128("IJ", j), u2, False, False)
            mm(blk("QP", j), v("IP"), pp, False, j == 15)
        act(v("DF", 0, 768), ind(v("X", 0, 4096), v("HU", 0, 48)), AF.Copy)
        mm(v("FC"), v("IB"), v("DF", 0, 512), True, False)
        mm(v("FC"), v("NB"), v("A2"), False, True)
        mm(v("TP", 0, 256), v("IB"), v("DF", 512, 768), True, False)
        mm(v("TP", 0, 256), v("NB"), v("A2", 0, 256), False, True)
        for i in range(1, 8):
            sl = (512 * i, 512 * i + 512) if i > 1 else (768, 1024)
            tt(v("DF", *sl), ind(v("X", 0, 4096), v("HU", sl[0] // 16, sl[1] // 16)), v("A2", 0, sl[1] - sl[0]), A.subtract)
            act(v("AB", *sl), v("DF", *sl), AF.Abs)
            if i == 2:
                act(v("AB", 0, 512), v("FC"), AF.Abs)
                act(v("AB", 512, 768), v("TP", 0, 256), AF.Abs)
            if i in (2, 3, 5, 7):
                c = i // 2 if i != 2 else 0
                o = v("Y0", 64 * c, 64 * c + 64) if c < 3 else v("Y1", 0, 64)
                mm(o, v("BG"), v("MB"), True, False)
                for y in range(16):
                    mm(o, m128("EN", y), ("AB", 1024 * c + y, 1024 * c + 1024, 16), False, y == 15)
        mm(v("BPS", 0, 256), v("NB"), v(P), True, False)
        if t == 0:
            for y in range(16):
                act(m128("TR", y), m128("EN", y), AF.Copy, scale=v("LT16", y, y + 1))
        for h in halves:
            tt(v("KN", *h), v("QP", *h), v("HI", *h), A.add)
        filler(1)
        for h in halves:
            ts(v("UU", *h), v("KN", *h), 0xFFFFFF, A.bitwise_and)
        filler(1)
        tt(v("TM", 0, 128), v("UU", 0, 128), v("UU", 128, 256), A.min)
        ts(v("SF"), sc, 2048.0, A.add)
        filler(1)
        tt(v("TM", 128, 192), v("TM", 0, 64), v("TM", 64, 128), A.min)
        tt(v("SM", 0, 192), v("KN", 0, 192), v("Y0", 0, 192), A.min)
        tt(v("TM", 192, 224), v("TM", 128, 160), v("TM", 160, 192), A.min)
        tt(v("TX", 0, 96), v("SM", 0, 96), v("SM", 96, 192), A.max)
        tt(v("TM", 224, 240), v("TM", 192, 208), v("TM", 208, 224), A.min)
        tt(v("TX", 96, 144), v("TX", 0, 48), v("TX", 48, 96), A.max)
        ts(v("HPC"), v("TM", 224, 240), -10240.0, A.add)
        spread("TP", v("HPC"))
        tt(v("TX", 144, 160), v("TX", 96, 112), v("TX", 112, 128), A.max)
        ts(v("HP"), v("TM", 224, 240), -8192.0, A.add)
        tt(v("TX", 160, 176), v("TX", 128, 144), v("TX", 144, 160), A.max)
        cp(v("HKU"), v("HP"))
        act(v("XG"), ind(v("X", 0, 4096), v("HKU")), AF.Copy)
        mm(v("QP", 256, 512), v("IB"), v("XG"), True, False)
        mm(v("QP", 256, 512), v("IB"), v("A2", 0, 256), False, True)
        act(v("NHK"), v("HP"), AF.Copy, scale=-1.0)
        tt(v("SM", 192, 256), v("KN", 192, 256), v("Y1", 0, 64), A.min)
        tt(v("TX", 176, 192), v("TX", 160, 176), v("HP"), A.max)
        tt(v("TX", 192, 224), v("SM", 192, 224), v("SM", 224, 256), A.max)
        ts(v("WB"), v("SF"), 32.0, A.mult, float((25952 * t) % 131072 - 262144), A.add)
        tt(v("TX", 224, 240), v("TX", 192, 208), v("TX", 176, 192), A.max)
        filler(1)
        tt(v("MM"), v("TX", 208, 224), v("TX", 224, 240), A.max)
        filler(99)
        nsc, nu2, npp = [v(so, 16 * i, 16 * i + 16) for i in range(3)]
        ts(v("HK"), v("MM"), 4095, A.bitwise_and)
        ts(v("DL"), v("MM"), 14, A.arith_shift_right)
        tt(v("BP"), v("SF"), v("HK"), A.mult)
        tt(v("KS"), pp, v("DL"), A.add)
        tt(v("BZ"), v("BP"), v("WB"), A.add)
        ts(v("MI"), v("MM"), 8192.0, A.is_lt, 2.0, A.mult)
        act(v("W1"), v("KS"), AF.Copy, scale=-1.0, bias=7.0)
        act(v("W3"), v("KS"), AF.Copy, bias=1.0)
        ts(v("BI"), v("BZ"), 5, A.arith_shift_right, 4095, A.bitwise_and)
        ts(v("KQ"), v("KS"), 15.0, A.is_equal, 2.0, A.mult)
        ts(v("BC"), v("BI"), -2048.0, A.add)
        for j in range(16):
            mm(blk("BPS", j), v("IB"), v("BC"), False, j == 15)
        if not last:
            mm(v("Y0", 256, 272), v("HF"), v("MI"))
        tt(v("TU"), v("KQ"), v("MI"), A.max)
        ts(v("TQ0"), v("MM"), 8192.0, A.is_ge, -12000.0, A.mult)
        tt(v("UN"), u2, v("TU"), A.not_equal)
        tt(v("W2"), v("W1"), v("TU"), A.mult)
        ts(nu2, v("UN"), 2.0, A.mult)
        tt(npp, v("W2"), v("W3"), A.add)
        ts(nsc, v("HK"), -2048.0, A.add)
        if not last:
            remote(nxt, "S%d" % (t + 1), so, "rS%d" % (t + 1), "lS%d" % (t + 1))
        tt(v("TQ"), v("TQ0"), v("HPC"), A.add)
        cp(v("TS"), v("TP", 0, 256))
        for b in on_scalar:
            act(v("ET", 272 * b, 256 * b + 256), v("TP", 16 * b, 256), AF.Abs, scale=-1.0, bias=v("TQ", b, b + 1))
        for b in on_scalar:
            act(v("EQ", 272 * b, 256 * b + 256), v("ET", 272 * b, 256 * b + 256), AF.Relu, scale=-1.0, bias=1.0)
        if not last:
            act(v("MJ"), v("Y0", 256, 272), AF.Copy, accum=v("MC", 0, 1))
        ts(v("LIM"), v("DL"), 16384.0, A.mult, 16383.0, A.add)

        def names():
            tt(v("MK"), ind(v("LIM"), v("LB")), v("UU"), A.is_ge)
            for lo in (0, 128):
                tt(v("BPS", 256 + lo, 384 + lo), v("BPS", lo, lo + 128), v("MK", lo, lo + 128), A.mult)
            for lo in (0, 128):
                tt(v(po, lo, lo + 128), v("BPS", 256 + lo, 384 + lo), v(P, lo, lo + 128), A.add)

        def compare(bs):
            for b in bs:
                if b not in on_scalar:
                    ts(v("EQ", 272 * b, 256 * b + 256), v("TS", 16 * b, 256), v("TQ", b, b + 1), A.is_equal)
                if b < 15:
                    mm(v("FC", 16 * b + 16, 256), v("BO"), v("EQ", 272 * b + 16, 256 * b + 256), b == 0, b == order[-1])

        if last:
            compare(order)
            names()
            cp(v("LP"), v(po))
        else:
            compare(order[:1])
            names()
            remote(nxt, "P%d" % (t + 1), po, "rP%d" % (t + 1), "lP%d" % (t + 1))
            compare(order[1:])
        act(v("VB"), v("QP", 256, 512), AF.Copy, bias=191.75, scale=0.5)
        act(v("FS", 16, 256), v("FC", 16, 256), AF.Copy)
        if t == 0:
            fill(v("FS", 0, 16), 0.0)
        for y in range(16):
            mm(v("Y1", 256, 272), m128("TR", y), ("EQ", y, y + 4081, 272), y == 0, False)
        for y in range(16):
            mm(v("Y1", 256, 272), m128("EN", y), ("FS", y, 256, 16), False, y == 15)
        tt(v("O1"), v("TQ0"), v("NDUM"), A.max)
        if not last:
            tt(v("O1"), v("O1"), v("NHK"), A.min)
            cp(v("MCI", 0, 1), v("MC", 0, 1))
            ts(v("MCI", 1, 2), v("MCI", 0, 1), 15, A.bitwise_and)
            cp(v("MC", 1, 2), v("MCI", 1, 2))
            act(v("MB"), v("C63"), AF.Identity, bias=v("MC", 1, 2))
        else:
            tt(v("O1"), v("O1"), v("NHK"), A.min)
        if t == 1:
            output_lists()
        if t == 0:
            key_matrices()
        tt(v("O2"), v("Y1", 256, 272), v("NDUM"), A.max)
        tt(v("O3"), v("O2"), v("O1"), A.min)
        ts(v("OU"), v("O3"), -1.0, A.mult)
        tt(ind(v("X"), v("OU")), v("VB"), v("CN"), A.add)
        if last:
            dma("S", "d6", lambda q: q.dma_start(T.yx[:, :], T.X[:, 0:4096]), [v("X", 0, 4096)], [])
            ts(v("W1"), nu2, 8.0, A.mult, -2048.0, A.add)
            cp(v("LX", 256, 272), nsc)
            tt(v("LX", 272, 288), v("W1"), npp, A.add)
            tt(v("SM"), ind(v("LP"), v("LREV")), v(po), A.subtract)
            tt(v("TM"), ind(v("UN"), v("LB")), v("SM"), A.mult)
            tt(v("LX", 0, 256), v("TM"), v("LP"), A.add)
            cp(v("T1"), ind(v("LX"), v("LL3")))
            tp(v("T2"), v("T1"))
            ts(v("KX"), ind(v("T2"), v("LL4")), 2048.0, A.add)
            dma("A", "d7", lambda q: q.dma_start(T.ys[:, :], T.KX[:, 256:272]), [v("KX", 256, 272)], [])
            dma("S", "d8", lambda q: q.dma_start(T.yp[:, :], T.KX[:, 272:288]), [v("KX", 272, 288)], [])
            dma("A", "d9", lambda q: q.dma_start(T.yn[:, :], T.KX[:, 0:256]), [v("KX", 0, 256)], [])
    finish()
